import numpy as np
import ml_dtypes


def mxq(x, axis, fmt="e4m3"):
    dtype, down = {"e4m3": (ml_dtypes.float8_e4m3fn, 7), "e5m2": (ml_dtypes.float8_e5m2, 14)}[fmt]
    v = np.moveaxis(np.asarray(x, np.float32).astype(ml_dtypes.bfloat16).astype(np.float64), axis, -1)
    blocks = v.reshape(v.shape[:-1] + (-1, 32))
    amax = np.abs(blocks).max(-1, keepdims=True)
    byte = np.maximum(np.where(amax > 0, np.frexp(amax)[1] - 1 + 127, 0) - down, 1)
    scale = np.exp2(byte - 127.0)
    codes = (blocks / scale).astype(np.float32).astype(dtype).astype(np.float64)
    return np.moveaxis((codes * scale).reshape(v.shape), -1, axis)


WIDE = False


def mx_kscale(k):
    if not WIDE:
        return np.ones(k)
    levels = np.array([24, -24, 12, -12, 0])
    if k % 512:
        return np.exp2(np.random.permutation(np.resize(levels, k // 32))).repeat(32)
    a = np.empty((k // 512, 16))
    for p in range(k // 512):
        a[p, :8] = np.random.permutation(np.resize(levels, 8))
        for g in range(8):
            far = levels[np.abs(levels - a[p, g]) >= 10]
            a[p, g + 8] = far[np.random.randint(len(far))]
    return np.exp2(a.ravel()).repeat(32)


def f64(x):
    return np.asarray(x).astype(np.float64)


def striped(idx):
    return np.tile(idx.reshape(-1, 16).T, (8, 1)).astype(np.uint16)


def unstriped(offs):
    return offs[:16].T.reshape(-1).astype(np.int64)


E2M1 = np.array([0.0, 0.5, 1.0, 1.5, 2.0, 3.0, 4.0, 6.0, -0.0, -0.5, -1.0, -1.5, -2.0, -3.0, -4.0, -6.0])


def pack_weight(w, fmt):
    k, n = w.shape
    w = f64(np.asarray(w, np.float32).astype(ml_dtypes.bfloat16)).reshape(k // 32, 32, n)
    amax = np.abs(w).max(1)
    if fmt == "e4m3":
        byte = np.frexp(amax)[1] - 1 + 127 - 7
    else:
        mant, ex = np.frexp(amax / 6.0)
        byte = np.where(mant > 0.5, ex, ex - 1) + 127
    byte = np.clip(np.where(amax > 0, byte, 1), 1, 254)
    scaled = (w * np.exp2(127.0 - byte)[:, None, :]).reshape(k, n).astype(np.float32)
    by_word = np.ascontiguousarray(scaled.reshape(k // 512, 128, 4, n).transpose(0, 1, 3, 2))
    if fmt == "e4m3":
        words = by_word.astype(ml_dtypes.float8_e4m3fn).view(np.uint8)
    else:
        c = by_word.astype(ml_dtypes.float4_e2m1fn).view(np.uint8) & 0xF
        words = (c[..., 0::2] | (c[..., 1::2] << 4)).reshape(k // 512, 128, 2 * n)
    return np.ascontiguousarray(words), np.ascontiguousarray(byte.astype(np.uint8).reshape(k // 512, 16, n))


def unpack_weight(words, scales, fmt):
    g, _, n = scales.shape
    words = np.ascontiguousarray(words).reshape(g, 128, n, -1)
    if fmt == "e4m3":
        vals = words.view(ml_dtypes.float8_e4m3fn).astype(np.float64)
    else:
        nib = np.empty((g, 128, n, 4), np.uint8)
        nib[..., 0::2] = words & 0xF
        nib[..., 1::2] = words >> 4
        vals = E2M1[nib]
    vals = vals * np.repeat(np.exp2(scales.astype(np.float64) - 127.0), 8, axis=1)[..., None]
    return vals.transpose(0, 1, 3, 2).reshape(g * 512, n)


K, M, N, J, T = 512, 1024, 256, 1024, 4096


def setup_inputs():
    n = np.random.standard_normal
    s = mx_kscale(K)[:, None]
    u = mx_kscale(J)[:, None]
    p_tab = pack_weight(0.5 * n((K, T)) / np.sqrt(K) / s, "e4m3")
    p_al = pack_weight(n((J, N)) / np.sqrt(J) / u, "e2m1")
    return {
        "x": (n((K, M)) * s).astype(np.float32),
        "tab_words": p_tab[0],
        "tab_scales": p_tab[1],
        "cw": (np.random.uniform(0.5, 2.0, J) * u[:, 0]).astype(np.float32),
        "cb": (0.3 * n(J)).astype(np.float32),
        "al_words": p_al[0],
        "al_scales": p_al[1],
        "b": (0.3 * n(N)).astype(np.float32),
        "offs": striped(np.random.permutation(T)[:J]),
    }


def reference(x, tab_words, tab_scales, cw, cb, al_words, al_scales, b, offs):
    idx = unstriped(offs)
    x_ = mxq(f64(x), 0, "e4m3")
    tab_ = unpack_weight(tab_words, tab_scales, "e4m3")[:, idx]
    d = tab_.T @ x_
    h = f64(cw)[:, None] * np.maximum(d + f64(cb)[:, None], 0.0)
    h_ = mxq(h, 0, "e4m3")
    al_ = unpack_weight(al_words, al_scales, "e2m1")
    y = al_.T @ h_
    return y + f64(b)[:, None]

@@ -1,0 +1,201 @@
+from contextlib import ExitStack
+
+import concourse.mybir as mybir
+
+K, M, N, J, T = 512, 1024, 256, 1024, 4096
+FLOPS = 2 * K * J * M + 2 * J * N * M
+
+F32 = mybir.dt.float32
+BF16 = mybir.dt.bfloat16
+I32 = mybir.dt.int32
+U32 = mybir.dt.uint32
+U16 = mybir.dt.uint16
+U8 = mybir.dt.uint8
+FP8X4 = mybir.dt.float8_e4m3fn_x4
+FP4X4 = mybir.dt.float4_e2m1fn_x4
+ALU = mybir.AluOpType
+ACT = mybir.ActivationFunctionType
+
+P = 128
+PACK = 4
+PASS = P * PACK
+PASSES = J // PASS
+BANK = 512
+CHUNKS = [(0, 256), (256, 512), (768, 256)]
+
+
+def tile_list_kernl_arc_bias_kernel(tc, x, tab_words, tab_scales, cw, cb, al_words, al_scales, b, offs, out):
+    nc = tc.nc
+    with ExitStack() as ctx:
+        keep = ctx.enter_context(tc.tile_pool(name="keep", bufs=1))
+        psum_d = ctx.enter_context(tc.psum_pool(name="psum_d", bufs=6))
+        psum_y = ctx.enter_context(tc.psum_pool(name="psum_y", bufs=2))
+
+        offsets = keep.tile([P, J // 16], U16, name="offsets")
+        nc.sync.dma_start(offsets[:], offs)
+
+        tscale = keep.tile([P, T], U8, name="tscale", align_bytes=64)
+        nc.vector.memset(tscale[:].bitcast(I32), 0)
+        ascale = keep.tile([P, PASSES, N], U8, name="ascale", align_bytes=64)
+        nc.vector.memset(ascale[:].rearrange("p a n -> p (a n)").bitcast(I32), 0)
+        for q in range(4):
+            nc.scalar.dma_start(tscale[32 * q : 32 * q + 4, :].bitcast(I32), tab_scales[0, 4 * q : 4 * q + 4, :].bitcast(I32))
+
+        x_rows = x.rearrange("(p i) m -> p i m", i=PACK)
+        raw = [keep.tile([P, PACK, w], F32, name=f"raw{c}") for c, (m0, w) in enumerate(CHUNKS)]
+        table = keep.tile([P, T], I32, name="table", align_bytes=64)
+        nc.sync.dma_start(raw[0][:], x_rows[:, :, 0 : CHUNKS[0][1]])
+        nc.sync.dma_start(table[:], tab_words[0].rearrange("p t i -> p (t i)").bitcast(I32))
+        for c in range(1, len(CHUNKS)):
+            m0, w = CHUNKS[c]
+            nc.sync.dma_start(raw[c][:], x_rows[:, :, m0 : m0 + w])
+
+        cw_t = keep.tile([P, PASSES, PACK], F32, name="cw_t")
+        cb_t = keep.tile([P, PASSES, PACK], F32, name="cb_t")
+        b_t = keep.tile([P, N // P], F32, name="b_t")
+        al_t = keep.tile([P, PASSES, 2 * N], U8, name="al_t", align_bytes=64)
+        nc.gpsimd.dma_start(cw_t[:], cw.rearrange("(a p t) -> p a t", p=P, t=PACK))
+        nc.gpsimd.dma_start(cb_t[:], cb.rearrange("(a p t) -> p a t", p=P, t=PACK))
+        nc.gpsimd.dma_start(al_t[:].bitcast(I32), al_words.rearrange("a p n -> p a n").bitcast(I32))
+        for q in range(4):
+            nc.gpsimd.dma_start(
+                ascale[32 * q : 32 * q + 4, :, :].bitcast(I32),
+                al_scales[:, 4 * q : 4 * q + 4, :].rearrange("a r n -> r a n").bitcast(I32),
+            )
+        with nc.allow_non_contiguous_dma(reason="one bias value a partition"):
+            nc.gpsimd.dma_start(b_t[:], b.rearrange("(c p) -> p c", p=P))
+
+        warm = keep.tile([P, 1], F32, name="warm")
+        nc.vector.memset(warm[:], 0.0)
+        warm_out = keep.tile([P, 1], F32, name="warm_out")
+        nc.scalar.activation(warm_out[:], warm[:], ACT.Relu)
+
+        half = keep.tile([P, PASSES * PACK], F32, name="half")
+        sign = keep.tile([P, PASSES * PACK], F32, name="sign")
+        gain = keep.tile([P, PASSES * PACK], F32, name="gain")
+        shift = keep.tile([P, PASSES * PACK], F32, name="shift")
+        cw_f = cw_t[:].rearrange("p a t -> p (a t)")
+        cb_f = cb_t[:].rearrange("p a t -> p (a t)")
+        nc.gpsimd.tensor_scalar(half[:], cw_f, 0.0, 2.0, ALU.is_ge, ALU.mult)
+        nc.gpsimd.tensor_scalar(sign[:], half[:], 1.0, -1.0, ALU.mult, ALU.add)
+        nc.gpsimd.tensor_tensor(gain[:], cw_f, sign[:], ALU.mult)
+        nc.gpsimd.tensor_tensor(shift[:], gain[:], cb_f, ALU.mult)
+
+        picked_scale = keep.tile([P, J], U8, name="picked_scale", align_bytes=64)
+        nc.vector.tensor_copy(picked_scale[:], tscale[:].indirect(offsets[:]))
+        v_scale = keep.tile([P, J], U8, name="v_scale", align_bytes=64)
+        nc.vector.tensor_copy(
+            v_scale[:].rearrange("p (a t q) -> p a t q", a=PASSES, t=PACK),
+            picked_scale[:].rearrange("p (a q t) -> p a t q", a=PASSES, t=PACK),
+        )
+
+        x_codes, x_scale = [], []
+
+        def quantize_x(c, engine):
+            w = CHUNKS[c][1]
+            grouped = keep.tile([P, w * PACK], BF16, name=f"xg{c}", align_bytes=64)
+            dst = grouped[:].rearrange("p (c i t) -> p c t i", i=4, t=PACK)
+            src = raw[c][:].rearrange("p t (c i) -> p c t i", i=4)
+            if engine == "scalar":
+                nc.scalar.copy(dst, src)
+            else:
+                nc.vector.tensor_copy(dst, src)
+            codes = keep.tile([P, w], U32, name=f"xc{c}", align_bytes=64)
+            scale = keep.tile([P, w], U8, name=f"xs{c}", align_bytes=64)
+            nc.vector.quantize_mx(codes[:].bitcast(FP8X4), scale[:], grouped[:])
+            x_codes.append(codes)
+            x_scale.append(scale)
+
+        quantize_x(0, "scalar")
+
+        v_codes = []
+        for a in range(PASSES):
+            codes = keep.tile([P, PACK, P], U32, name=f"vc{a}", align_bytes=64)
+            cols = PASS // 16
+            nc.vector.tensor_copy(
+                codes[:].rearrange("p t q -> p q t"),
+                table[:].bitcast(U32).indirect(offsets[:, a * cols : (a + 1) * cols]),
+            )
+            v_codes.append(codes)
+
+        planes = {}
+        h_mx = {}
+
+        def first_stage(c, a):
+            w = CHUNKS[c][1]
+            plane = keep.tile([P, PACK, w], BF16, name=f"hp{c}_{a}", align_bytes=64)
+            for t in range(PACK):
+                d = psum_d.tile([P, BANK], F32, name="d")
+                col = a * PACK + t
+                nc.tensor.matmul_mx(
+                    d[:, 0:w],
+                    lhsT=v_codes[a][:, t, :].bitcast(FP8X4),
+                    lhsT_scale=v_scale[:, col * P : (col + 1) * P],
+                    rhs=x_codes[c][:].bitcast(FP8X4),
+                    rhs_scale=x_scale[c][:],
+                    start=True,
+                    stop=True,
+                )
+                nc.scalar.activation(
+                    plane[:, t, :], d[:, 0:w], ACT.Relu, bias=shift[:, col : col + 1], scale=gain[:, col : col + 1]
+                )
+            planes[c, a] = plane
+
+        def quantize_h(c, a):
+            w = CHUNKS[c][1]
+            plane = planes[c, a]
+            signed = keep.tile([P, PACK, w], BF16, name=f"hs{c}_{a}", align_bytes=64)
+            for t in range(PACK):
+                col = a * PACK + t
+                nc.vector.tensor_scalar(signed[:, t, :], plane[:, t, :], sign[:, col : col + 1], None, ALU.mult)
+            grouped = keep.tile([P, w * PACK], BF16, name=f"hg{c}_{a}", align_bytes=64)
+            nc.vector.tensor_copy(
+                grouped[:].rearrange("p (c i t) -> p c t i", i=4, t=PACK),
+                signed[:].rearrange("p t (c i) -> p c t i", i=4),
+            )
+            codes = keep.tile([P, w], U32, name=f"hc{c}_{a}", align_bytes=64)
+            scale = keep.tile([P, w], U8, name=f"hq{c}_{a}", align_bytes=64)
+            nc.vector.quantize_mx(codes[:].bitcast(FP8X4), scale[:], grouped[:])
+            h_mx[c, a] = (codes, scale)
+
+        def second_stage(c, last):
+            m0, w = CHUNKS[c]
+            step = BANK if w == BANK else P
+            result = keep.tile([P, N // P, w], F32, name=f"res{c}")
+            for g in range(N // P):
+                y = psum_y.tile([P, BANK], F32, name="y")
+                for s0 in range(0, w, step):
+                    for a in range(PASSES):
+                        codes, scale = h_mx[c, a]
+                        nc.tensor.matmul_mx(
+                            y[:, s0 : s0 + step],
+                            lhsT=al_t[:, a, 2 * P * g : 2 * P * (g + 1)].bitcast(FP4X4),
+                            lhsT_scale=ascale[:, a, P * g : P * (g + 1)],
+                            rhs=codes[:, s0 : s0 + step].bitcast(FP8X4),
+                            rhs_scale=scale[:, s0 : s0 + step],
+                            start=(a == 0),
+                            stop=(a == PASSES - 1),
+                        )
+                if last and g == 1:
+                    nc.vector.tensor_scalar(result[:, g, :], y[:, 0:w], b_t[:, g : g + 1], None, ALU.add)
+                else:
+                    nc.scalar.activation(result[:, g, :], y[:, 0:w], ACT.Identity, bias=b_t[:, g : g + 1])
+            nc.sync.dma_start(out.rearrange("(g p) m -> p g m", p=P)[:, :, m0 : m0 + w], result[:])
+
+        first_stage(0, 0)
+        quantize_x(1, "vector")
+        first_stage(0, 1)
+        quantize_h(0, 0)
+        first_stage(1, 0)
+        quantize_h(0, 1)
+        quantize_x(2, "scalar")
+        first_stage(1, 1)
+        quantize_h(1, 0)
+        second_stage(0, False)
+        first_stage(2, 0)
+        quantize_h(1, 1)
+        first_stage(2, 1)
+        quantize_h(2, 0)
+        second_stage(1, False)
+        quantize_h(2, 1)
+        second_stage(2, True)

@@ -21,34 +21,42 @@ PACK = 4
 PASS = P * PACK
 PASSES = J // PASS
 BANK = 512
-CHUNKS = [(0, 256), (256, 512), (768, 256)]
+HALF = M // 2
+LAST_PIECES = [(0, 256), (256, 128), (384, 128)]
 
 
 def tile_list_kernl_arc_bias_kernel(tc, x, tab_words, tab_scales, cw, cb, al_words, al_scales, b, offs, out):
     nc = tc.nc
     with ExitStack() as ctx:
         keep = ctx.enter_context(tc.tile_pool(name="keep", bufs=1))
-        psum_d = ctx.enter_context(tc.psum_pool(name="psum_d", bufs=6))
-        psum_y = ctx.enter_context(tc.psum_pool(name="psum_y", bufs=2))
+        psum_d = ctx.enter_context(tc.psum_pool(name="psum_d", bufs=4))
+        psum_y = ctx.enter_context(tc.psum_pool(name="psum_y", bufs=4))
 
         offsets = keep.tile([P, J // 16], U16, name="offsets")
         nc.sync.dma_start(offsets[:], offs)
+
+        warm = keep.tile([P, 1], F32, name="warm", tag="table", align_bytes=64)
+        nc.vector.memset(warm[:], 0.0)
+        warm_out = keep.tile([P, 1], F32, name="warm_out")
+        nc.scalar.activation(warm_out[:], warm[:], ACT.Relu)
 
         tscale = keep.tile([P, T], U8, name="tscale", align_bytes=64)
         nc.vector.memset(tscale[:].bitcast(I32), 0)
         ascale = keep.tile([P, PASSES, N], U8, name="ascale", align_bytes=64)
         nc.vector.memset(ascale[:].rearrange("p a n -> p (a n)").bitcast(I32), 0)
-        for q in range(4):
-            nc.scalar.dma_start(tscale[32 * q : 32 * q + 4, :].bitcast(I32), tab_scales[0, 4 * q : 4 * q + 4, :].bitcast(I32))
 
         x_rows = x.rearrange("(p i) m -> p i m", i=PACK)
-        raw = [keep.tile([P, PACK, w], F32, name=f"raw{c}") for c, (m0, w) in enumerate(CHUNKS)]
-        table = keep.tile([P, T], I32, name="table", align_bytes=64)
-        nc.sync.dma_start(raw[0][:], x_rows[:, :, 0 : CHUNKS[0][1]])
+
+        def load_x(h):
+            raw = keep.tile([P, PACK, HALF], F32, name="raw")
+            nc.sync.dma_start(raw[:], x_rows[:, :, h * HALF : (h + 1) * HALF])
+            return raw
+
+        raw_first = load_x(0)
+        for q in range(4):
+            nc.sync.dma_start(tscale[32 * q : 32 * q + 4, :].bitcast(I32), tab_scales[0, 4 * q : 4 * q + 4, :].bitcast(I32))
+        table = keep.tile([P, T], I32, name="table", tag="table", align_bytes=64)
         nc.sync.dma_start(table[:], tab_words[0].rearrange("p t i -> p (t i)").bitcast(I32))
-        for c in range(1, len(CHUNKS)):
-            m0, w = CHUNKS[c]
-            nc.sync.dma_start(raw[c][:], x_rows[:, :, m0 : m0 + w])
 
         cw_t = keep.tile([P, PASSES, PACK], F32, name="cw_t")
         cb_t = keep.tile([P, PASSES, PACK], F32, name="cb_t")
@@ -56,6 +64,18 @@ def tile_list_kernl_arc_bias_kernel(tc, x, tab_words, tab_scales, cw, cb, al_wor
         al_t = keep.tile([P, PASSES, 2 * N], U8, name="al_t", align_bytes=64)
         nc.gpsimd.dma_start(cw_t[:], cw.rearrange("(a p t) -> p a t", p=P, t=PACK))
         nc.gpsimd.dma_start(cb_t[:], cb.rearrange("(a p t) -> p a t", p=P, t=PACK))
+
+        half = keep.tile([P, PASSES * PACK], F32, name="half")
+        sign = keep.tile([P, PASSES * PACK], F32, name="sign")
+        gain = keep.tile([P, PASSES * PACK], F32, name="gain")
+        shift = keep.tile([P, PASSES * PACK], F32, name="shift")
+        cw_f = cw_t[:].rearrange("p a t -> p (a t)")
+        cb_f = cb_t[:].rearrange("p a t -> p (a t)")
+        nc.vector.tensor_scalar(half[:], cw_f, 0.0, 2.0, ALU.is_ge, ALU.mult)
+        nc.vector.tensor_scalar(sign[:], half[:], 1.0, -1.0, ALU.mult, ALU.add)
+        nc.vector.tensor_tensor(gain[:], cw_f, sign[:], ALU.mult)
+        nc.vector.tensor_tensor(shift[:], gain[:], cb_f, ALU.mult)
+
         nc.gpsimd.dma_start(al_t[:].bitcast(I32), al_words.rearrange("a p n -> p a n").bitcast(I32))
         for q in range(4):
             nc.gpsimd.dma_start(
@@ -65,23 +85,7 @@ def tile_list_kernl_arc_bias_kernel(tc, x, tab_words, tab_scales, cw, cb, al_wor
         with nc.allow_non_contiguous_dma(reason="one bias value a partition"):
             nc.gpsimd.dma_start(b_t[:], b.rearrange("(c p) -> p c", p=P))
 
-        warm = keep.tile([P, 1], F32, name="warm")
-        nc.vector.memset(warm[:], 0.0)
-        warm_out = keep.tile([P, 1], F32, name="warm_out")
-        nc.scalar.activation(warm_out[:], warm[:], ACT.Relu)
-
-        half = keep.tile([P, PASSES * PACK], F32, name="half")
-        sign = keep.tile([P, PASSES * PACK], F32, name="sign")
-        gain = keep.tile([P, PASSES * PACK], F32, name="gain")
-        shift = keep.tile([P, PASSES * PACK], F32, name="shift")
-        cw_f = cw_t[:].rearrange("p a t -> p (a t)")
-        cb_f = cb_t[:].rearrange("p a t -> p (a t)")
-        nc.gpsimd.tensor_scalar(half[:], cw_f, 0.0, 2.0, ALU.is_ge, ALU.mult)
-        nc.gpsimd.tensor_scalar(sign[:], half[:], 1.0, -1.0, ALU.mult, ALU.add)
-        nc.gpsimd.tensor_tensor(gain[:], cw_f, sign[:], ALU.mult)
-        nc.gpsimd.tensor_tensor(shift[:], gain[:], cb_f, ALU.mult)
-
-        picked_scale = keep.tile([P, J], U8, name="picked_scale", align_bytes=64)
+        picked_scale = keep.tile([P, J], U8, name="picked_scale", tag="xs0", align_bytes=64)
         nc.vector.tensor_copy(picked_scale[:], tscale[:].indirect(offsets[:]))
         v_scale = keep.tile([P, J], U8, name="v_scale", align_bytes=64)
         nc.vector.tensor_copy(
@@ -91,22 +95,22 @@ def tile_list_kernl_arc_bias_kernel(tc, x, tab_words, tab_scales, cw, cb, al_wor
 
         x_codes, x_scale = [], []
 
-        def quantize_x(c, engine):
-            w = CHUNKS[c][1]
-            grouped = keep.tile([P, w * PACK], BF16, name=f"xg{c}", align_bytes=64)
-            dst = grouped[:].rearrange("p (c i t) -> p c t i", i=4, t=PACK)
-            src = raw[c][:].rearrange("p t (c i) -> p c t i", i=4)
-            if engine == "scalar":
-                nc.scalar.copy(dst, src)
-            else:
-                nc.vector.tensor_copy(dst, src)
-            codes = keep.tile([P, w], U32, name=f"xc{c}", align_bytes=64)
-            scale = keep.tile([P, w], U8, name=f"xs{c}", align_bytes=64)
-            nc.vector.quantize_mx(codes[:].bitcast(FP8X4), scale[:], grouped[:])
+        def quantize_x(c, raw, vector_cols):
+            grouped = keep.tile([P, HALF, PACK], BF16, name=f"xg{c}", align_bytes=64)
+            for engine, m0, m1 in ((nc.vector.tensor_copy, 0, vector_cols), (nc.scalar.copy, vector_cols, HALF)):
+                if m1 > m0:
+                    engine(
+                        grouped[:, m0:m1, :].rearrange("p (c i) t -> p c t i", i=4),
+                        raw[:, :, m0:m1].rearrange("p t (c i) -> p c t i", i=4),
+                    )
+            codes = keep.tile([P, HALF], U32, name=f"xc{c}", align_bytes=64)
+            scale = keep.tile([P, HALF], U8, name=f"xs{c}", tag=f"xs{c}", align_bytes=64)
+            nc.vector.quantize_mx(codes[:].bitcast(FP8X4), scale[:], grouped[:].rearrange("p m t -> p (m t)"))
             x_codes.append(codes)
             x_scale.append(scale)
 
-        quantize_x(0, "scalar")
+        quantize_x(0, raw_first, 0)
+        raw_second = load_x(1)
 
         v_codes = []
         for a in range(PASSES):
@@ -122,13 +126,12 @@ def tile_list_kernl_arc_bias_kernel(tc, x, tab_words, tab_scales, cw, cb, al_wor
         h_mx = {}
 
         def first_stage(c, a):
-            w = CHUNKS[c][1]
-            plane = keep.tile([P, PACK, w], BF16, name=f"hp{c}_{a}", align_bytes=64)
+            plane = keep.tile([P, PACK, HALF], BF16, name=f"hp{c}_{a}", align_bytes=64)
             for t in range(PACK):
                 d = psum_d.tile([P, BANK], F32, name="d")
                 col = a * PACK + t
                 nc.tensor.matmul_mx(
-                    d[:, 0:w],
+                    d[:],
                     lhsT=v_codes[a][:, t, :].bitcast(FP8X4),
                     lhsT_scale=v_scale[:, col * P : (col + 1) * P],
                     rhs=x_codes[c][:].bitcast(FP8X4),
@@ -137,42 +140,43 @@ def tile_list_kernl_arc_bias_kernel(tc, x, tab_words, tab_scales, cw, cb, al_wor
                     stop=True,
                 )
                 nc.scalar.activation(
-                    plane[:, t, :], d[:, 0:w], ACT.Relu, bias=shift[:, col : col + 1], scale=gain[:, col : col + 1]
+                    plane[:, t, :], d[:], ACT.Relu, bias=shift[:, col : col + 1], scale=gain[:, col : col + 1]
                 )
             planes[c, a] = plane
 
-        def quantize_h(c, a):
-            w = CHUNKS[c][1]
-            plane = planes[c, a]
-            signed = keep.tile([P, PACK, w], BF16, name=f"hs{c}_{a}", align_bytes=64)
+        def apply_sign(c, a):
+            signed = keep.tile([P, PACK, HALF], BF16, name=f"hs{c}_{a}", align_bytes=64)
             for t in range(PACK):
                 col = a * PACK + t
-                nc.vector.tensor_scalar(signed[:, t, :], plane[:, t, :], sign[:, col : col + 1], None, ALU.mult)
-            grouped = keep.tile([P, w * PACK], BF16, name=f"hg{c}_{a}", align_bytes=64)
+                nc.vector.tensor_scalar(signed[:, t, :], planes[c, a][:, t, :], sign[:, col : col + 1], None, ALU.mult)
+            planes[c, a] = signed
+
+        def quantize_h(c, a, m0, w):
+            grouped = keep.tile([P, w * PACK], BF16, name=f"hg{c}_{a}_{m0}", align_bytes=64)
             nc.vector.tensor_copy(
                 grouped[:].rearrange("p (c i t) -> p c t i", i=4, t=PACK),
-                signed[:].rearrange("p t (c i) -> p c t i", i=4),
+                planes[c, a][:, :, m0 : m0 + w].rearrange("p t (c i) -> p c t i", i=4),
             )
-            codes = keep.tile([P, w], U32, name=f"hc{c}_{a}", align_bytes=64)
-            scale = keep.tile([P, w], U8, name=f"hq{c}_{a}", align_bytes=64)
+            codes = keep.tile([P, w], U32, name=f"hc{c}_{a}_{m0}", align_bytes=64)
+            scale = keep.tile([P, w], U8, name=f"hq{c}_{a}_{m0}", align_bytes=64)
             nc.vector.quantize_mx(codes[:].bitcast(FP8X4), scale[:], grouped[:])
-            h_mx[c, a] = (codes, scale)
+            h_mx[c, a] = (codes, scale, m0)
 
-        def second_stage(c, last):
-            m0, w = CHUNKS[c]
+        def second_stage(c, m0, w, last):
             step = BANK if w == BANK else P
-            result = keep.tile([P, N // P, w], F32, name=f"res{c}")
+            result = keep.tile([P, N // P, w], F32, name=f"res{c}_{m0}")
             for g in range(N // P):
                 y = psum_y.tile([P, BANK], F32, name="y")
                 for s0 in range(0, w, step):
                     for a in range(PASSES):
-                        codes, scale = h_mx[c, a]
+                        codes, scale, base = h_mx[c, a]
+                        cols = slice(m0 + s0 - base, m0 + s0 - base + step)
                         nc.tensor.matmul_mx(
                             y[:, s0 : s0 + step],
                             lhsT=al_t[:, a, 2 * P * g : 2 * P * (g + 1)].bitcast(FP4X4),
                             lhsT_scale=ascale[:, a, P * g : P * (g + 1)],
-                            rhs=codes[:, s0 : s0 + step].bitcast(FP8X4),
-                            rhs_scale=scale[:, s0 : s0 + step],
+                            rhs=codes[:, cols].bitcast(FP8X4),
+                            rhs_scale=scale[:, cols],
                             start=(a == 0),
                             stop=(a == PASSES - 1),
                         )
@@ -180,22 +184,22 @@ def tile_list_kernl_arc_bias_kernel(tc, x, tab_words, tab_scales, cw, cb, al_wor
                     nc.vector.tensor_scalar(result[:, g, :], y[:, 0:w], b_t[:, g : g + 1], None, ALU.add)
                 else:
                     nc.scalar.activation(result[:, g, :], y[:, 0:w], ACT.Identity, bias=b_t[:, g : g + 1])
-            nc.sync.dma_start(out.rearrange("(g p) m -> p g m", p=P)[:, :, m0 : m0 + w], result[:])
+            first = c * HALF + m0
+            nc.sync.dma_start(out.rearrange("(g p) m -> p g m", p=P)[:, :, first : first + w], result[:])
 
         first_stage(0, 0)
-        quantize_x(1, "vector")
+        quantize_x(1, raw_second, HALF)
         first_stage(0, 1)
-        quantize_h(0, 0)
+        apply_sign(0, 0)
+        quantize_h(0, 0, 0, HALF)
         first_stage(1, 0)
-        quantize_h(0, 1)
-        quantize_x(2, "scalar")
+        apply_sign(0, 1)
+        quantize_h(0, 1, 0, HALF)
         first_stage(1, 1)
-        quantize_h(1, 0)
-        second_stage(0, False)
-        first_stage(2, 0)
-        quantize_h(1, 1)
-        first_stage(2, 1)
-        quantize_h(2, 0)
-        second_stage(1, False)
-        quantize_h(2, 1)
-        second_stage(2, True)
+        apply_sign(1, 0)
+        quantize_h(1, 0, 0, HALF)
+        second_stage(0, 0, HALF, False)
+        apply_sign(1, 1)
+        for m0, w in LAST_PIECES:
+            quantize_h(1, 1, m0, w)
+            second_stage(1, m0, w, m0 + w == HALF)

@@ -21,8 +21,7 @@ PACK = 4
 PASS = P * PACK
 PASSES = J // PASS
 BANK = 512
-HALF = M // 2
-LAST_PIECES = [(0, 256), (256, 128), (384, 128)]
+CHUNKS = [(0, 256), (256, 512), (768, 256)]
 
 
 def tile_list_kernl_arc_bias_kernel(tc, x, tab_words, tab_scales, cw, cb, al_words, al_scales, b, offs, out):
@@ -40,43 +39,32 @@ def tile_list_kernl_arc_bias_kernel(tc, x, tab_words, tab_scales, cw, cb, al_wor
         warm_out = keep.tile([P, 1], F32, name="warm_out")
         nc.scalar.activation(warm_out[:], warm[:], ACT.Relu)
 
-        tscale = keep.tile([P, T], U8, name="tscale", align_bytes=64)
+        tscale = keep.tile([P, T], U8, name="tscale", tag="tscale", align_bytes=64)
         nc.vector.memset(tscale[:].bitcast(I32), 0)
         ascale = keep.tile([P, PASSES, N], U8, name="ascale", align_bytes=64)
         nc.vector.memset(ascale[:].rearrange("p a n -> p (a n)").bitcast(I32), 0)
 
         x_rows = x.rearrange("(p i) m -> p i m", i=PACK)
 
-        def load_x(h):
-            raw = keep.tile([P, PACK, HALF], F32, name="raw")
-            nc.sync.dma_start(raw[:], x_rows[:, :, h * HALF : (h + 1) * HALF])
+        def load_x(c, tag):
+            m0, w = CHUNKS[c]
+            raw = keep.tile([P, PACK, w], F32, name=f"raw{c}", tag=tag, align_bytes=64)
+            nc.sync.dma_start(raw[:], x_rows[:, :, m0 : m0 + w])
             return raw
-
-        raw_first = load_x(0)
-        for q in range(4):
-            nc.sync.dma_start(tscale[32 * q : 32 * q + 4, :].bitcast(I32), tab_scales[0, 4 * q : 4 * q + 4, :].bitcast(I32))
-        table = keep.tile([P, T], I32, name="table", tag="table", align_bytes=64)
-        nc.sync.dma_start(table[:], tab_words[0].rearrange("p t i -> p (t i)").bitcast(I32))
 
         cw_t = keep.tile([P, PASSES, PACK], F32, name="cw_t")
         cb_t = keep.tile([P, PASSES, PACK], F32, name="cb_t")
         b_t = keep.tile([P, N // P], F32, name="b_t")
         al_t = keep.tile([P, PASSES, 2 * N], U8, name="al_t", align_bytes=64)
-        nc.gpsimd.dma_start(cw_t[:], cw.rearrange("(a p t) -> p a t", p=P, t=PACK))
-        nc.gpsimd.dma_start(cb_t[:], cb.rearrange("(a p t) -> p a t", p=P, t=PACK))
+        nc.sync.dma_start(cw_t[:], cw.rearrange("(a p t) -> p a t", p=P, t=PACK))
+        nc.sync.dma_start(cb_t[:], cb.rearrange("(a p t) -> p a t", p=P, t=PACK))
 
-        half = keep.tile([P, PASSES * PACK], F32, name="half")
-        sign = keep.tile([P, PASSES * PACK], F32, name="sign")
-        gain = keep.tile([P, PASSES * PACK], F32, name="gain")
-        shift = keep.tile([P, PASSES * PACK], F32, name="shift")
-        cw_f = cw_t[:].rearrange("p a t -> p (a t)")
-        cb_f = cb_t[:].rearrange("p a t -> p (a t)")
-        nc.vector.tensor_scalar(half[:], cw_f, 0.0, 2.0, ALU.is_ge, ALU.mult)
-        nc.vector.tensor_scalar(sign[:], half[:], 1.0, -1.0, ALU.mult, ALU.add)
-        nc.vector.tensor_tensor(gain[:], cw_f, sign[:], ALU.mult)
-        nc.vector.tensor_tensor(shift[:], gain[:], cb_f, ALU.mult)
+        raw_first = load_x(0, "raw")
+        for q in range(4):
+            nc.sync.dma_start(tscale[32 * q : 32 * q + 4, :].bitcast(I32), tab_scales[0, 4 * q : 4 * q + 4, :].bitcast(I32))
+        table = keep.tile([P, T], I32, name="table", tag="table", align_bytes=64)
+        nc.sync.dma_start(table[:], tab_words[0].rearrange("p t i -> p (t i)").bitcast(I32))
 
-        nc.gpsimd.dma_start(al_t[:].bitcast(I32), al_words.rearrange("a p n -> p a n").bitcast(I32))
         for q in range(4):
             nc.gpsimd.dma_start(
                 ascale[32 * q : 32 * q + 4, :, :].bitcast(I32),
@@ -84,6 +72,7 @@ def tile_list_kernl_arc_bias_kernel(tc, x, tab_words, tab_scales, cw, cb, al_wor
             )
         with nc.allow_non_contiguous_dma(reason="one bias value a partition"):
             nc.gpsimd.dma_start(b_t[:], b.rearrange("(c p) -> p c", p=P))
+        nc.gpsimd.dma_start(al_t[:].bitcast(I32), al_words.rearrange("a p n -> p a n").bitcast(I32))
 
         picked_scale = keep.tile([P, J], U8, name="picked_scale", tag="xs0", align_bytes=64)
         nc.vector.tensor_copy(picked_scale[:], tscale[:].indirect(offsets[:]))
@@ -95,22 +84,40 @@ def tile_list_kernl_arc_bias_kernel(tc, x, tab_words, tab_scales, cw, cb, al_wor
 
         x_codes, x_scale = [], []
 
-        def quantize_x(c, raw, vector_cols):
-            grouped = keep.tile([P, HALF, PACK], BF16, name=f"xg{c}", align_bytes=64)
-            for engine, m0, m1 in ((nc.vector.tensor_copy, 0, vector_cols), (nc.scalar.copy, vector_cols, HALF)):
-                if m1 > m0:
-                    engine(
-                        grouped[:, m0:m1, :].rearrange("p (c i) t -> p c t i", i=4),
-                        raw[:, :, m0:m1].rearrange("p t (c i) -> p c t i", i=4),
-                    )
-            codes = keep.tile([P, HALF], U32, name=f"xc{c}", align_bytes=64)
-            scale = keep.tile([P, HALF], U8, name=f"xs{c}", tag=f"xs{c}", align_bytes=64)
+        x_grouped = {}
+
+        def cast_x(c, raw, copy, tag):
+            w = CHUNKS[c][1]
+            grouped = keep.tile([P, w, PACK], BF16, name=f"xg{c}", tag=tag, align_bytes=64)
+            copy(
+                grouped[:].rearrange("p (c i) t -> p c t i", i=4),
+                raw[:].rearrange("p t (c i) -> p c t i", i=4),
+            )
+            x_grouped[c] = grouped
+
+        def quantize_x(c):
+            w = CHUNKS[c][1]
+            grouped = x_grouped[c]
+            codes = keep.tile([P, w], U32, name=f"xc{c}", align_bytes=64)
+            scale = keep.tile([P, w], U8, name=f"xs{c}", tag=f"xs{c}", align_bytes=64)
             nc.vector.quantize_mx(codes[:].bitcast(FP8X4), scale[:], grouped[:].rearrange("p m t -> p (m t)"))
             x_codes.append(codes)
             x_scale.append(scale)
 
-        quantize_x(0, raw_first, 0)
-        raw_second = load_x(1)
+        cast_x(0, raw_first, nc.scalar.copy, "xg0")
+        quantize_x(0)
+        raw_second = load_x(1, "raw")
+        raw_third = load_x(2, "tscale")
+
+        sign = keep.tile([P, PASSES * PACK], F32, name="sign")
+        gain = keep.tile([P, PASSES * PACK], F32, name="gain")
+        shift = keep.tile([P, PASSES * PACK], F32, name="shift")
+        cw_f = cw_t[:].rearrange("p a t -> p (a t)")
+        cb_f = cb_t[:].rearrange("p a t -> p (a t)")
+        nc.scalar.activation(gain[:], cw_f, ACT.Abs)
+        nc.scalar.activation(sign[:], cw_f, ACT.Sign)
+        for col in range(PASSES * PACK):
+            nc.scalar.activation(shift[:, col : col + 1], cb_f[:, col : col + 1], ACT.Copy, scale=gain[:, col : col + 1])
 
         v_codes = []
         for a in range(PASSES):
@@ -126,12 +133,13 @@ def tile_list_kernl_arc_bias_kernel(tc, x, tab_words, tab_scales, cw, cb, al_wor
         h_mx = {}
 
         def first_stage(c, a):
-            plane = keep.tile([P, PACK, HALF], BF16, name=f"hp{c}_{a}", align_bytes=64)
+            w = CHUNKS[c][1]
+            plane = keep.tile([P, PACK, w], BF16, name=f"hp{c}_{a}", tag=f"hp{c}_{a}", align_bytes=64)
             for t in range(PACK):
                 d = psum_d.tile([P, BANK], F32, name="d")
                 col = a * PACK + t
                 nc.tensor.matmul_mx(
-                    d[:],
+                    d[:, 0:w],
                     lhsT=v_codes[a][:, t, :].bitcast(FP8X4),
                     lhsT_scale=v_scale[:, col * P : (col + 1) * P],
                     rhs=x_codes[c][:].bitcast(FP8X4),
@@ -140,26 +148,31 @@ def tile_list_kernl_arc_bias_kernel(tc, x, tab_words, tab_scales, cw, cb, al_wor
                     stop=True,
                 )
                 nc.scalar.activation(
-                    plane[:, t, :], d[:], ACT.Relu, bias=shift[:, col : col + 1], scale=gain[:, col : col + 1]
+                    plane[:, t, :], d[:, 0:w], ACT.Relu, bias=shift[:, col : col + 1], scale=gain[:, col : col + 1]
                 )
             planes[c, a] = plane
 
         def apply_sign(c, a):
-            signed = keep.tile([P, PACK, HALF], BF16, name=f"hs{c}_{a}", align_bytes=64)
+            signed = keep.tile([P, PACK, CHUNKS[c][1]], BF16, name=f"hs{c}_{a}", align_bytes=64)
             for t in range(PACK):
                 col = a * PACK + t
                 nc.vector.tensor_scalar(signed[:, t, :], planes[c, a][:, t, :], sign[:, col : col + 1], None, ALU.mult)
             planes[c, a] = signed
 
-        def quantize_h(c, a, m0, w):
+        h_grouped = {}
+
+        def interleave_h(c, a, m0, w):
             grouped = keep.tile([P, w * PACK], BF16, name=f"hg{c}_{a}_{m0}", align_bytes=64)
             nc.vector.tensor_copy(
                 grouped[:].rearrange("p (c i t) -> p c t i", i=4, t=PACK),
                 planes[c, a][:, :, m0 : m0 + w].rearrange("p t (c i) -> p c t i", i=4),
             )
+            h_grouped[c, a, m0] = grouped
+
+        def quantize_h(c, a, m0, w):
             codes = keep.tile([P, w], U32, name=f"hc{c}_{a}_{m0}", align_bytes=64)
             scale = keep.tile([P, w], U8, name=f"hq{c}_{a}_{m0}", align_bytes=64)
-            nc.vector.quantize_mx(codes[:].bitcast(FP8X4), scale[:], grouped[:])
+            nc.vector.quantize_mx(codes[:].bitcast(FP8X4), scale[:], h_grouped[c, a, m0][:])
             h_mx[c, a] = (codes, scale, m0)
 
         def second_stage(c, m0, w, last):
@@ -184,22 +197,40 @@ def tile_list_kernl_arc_bias_kernel(tc, x, tab_words, tab_scales, cw, cb, al_wor
                     nc.vector.tensor_scalar(result[:, g, :], y[:, 0:w], b_t[:, g : g + 1], None, ALU.add)
                 else:
                     nc.scalar.activation(result[:, g, :], y[:, 0:w], ACT.Identity, bias=b_t[:, g : g + 1])
-            first = c * HALF + m0
+            first = CHUNKS[c][0] + m0
             nc.sync.dma_start(out.rearrange("(g p) m -> p g m", p=P)[:, :, first : first + w], result[:])
 
         first_stage(0, 0)
-        quantize_x(1, raw_second, HALF)
+        cast_x(1, raw_second, nc.vector.tensor_copy, "table")
         first_stage(0, 1)
         apply_sign(0, 0)
-        quantize_h(0, 0, 0, HALF)
+        quantize_x(1)
+        interleave_h(0, 0, 0, 256)
         first_stage(1, 0)
         apply_sign(0, 1)
-        quantize_h(0, 1, 0, HALF)
+        quantize_h(0, 0, 0, 256)
+        interleave_h(0, 1, 0, 256)
+        cast_x(2, raw_third, nc.scalar.copy, "hp0_0")
         first_stage(1, 1)
+        quantize_x(2)
+        quantize_h(0, 1, 0, 256)
         apply_sign(1, 0)
-        quantize_h(1, 0, 0, HALF)
-        second_stage(0, 0, HALF, False)
+        second_stage(0, 0, 256, False)
+        interleave_h(1, 0, 0, 512)
+        first_stage(2, 0)
         apply_sign(1, 1)
-        for m0, w in LAST_PIECES:
-            quantize_h(1, 1, m0, w)
-            second_stage(1, m0, w, m0 + w == HALF)
+        quantize_h(1, 0, 0, 512)
+        interleave_h(1, 1, 0, 512)
+        first_stage(2, 1)
+        apply_sign(2, 0)
+        quantize_h(1, 1, 0, 512)
+        interleave_h(2, 0, 0, 256)
+        second_stage(1, 0, 512, False)
+        apply_sign(2, 1)
+        quantize_h(2, 0, 0, 256)
+        interleave_h(2, 1, 0, 128)
+        interleave_h(2, 1, 128, 128)
+        quantize_h(2, 1, 0, 128)
+        second_stage(2, 0, 128, False)
+        quantize_h(2, 1, 128, 128)
+        second_stage(2, 128, 128, True)

@@ -21,6 +21,7 @@ PACK = 4
 PASS = P * PACK
 PASSES = J // PASS
 BANK = 512
+UNIT = 256
 CHUNKS = [(0, 256), (256, 512), (768, 256)]
 
 
@@ -41,38 +42,23 @@ def tile_list_kernl_arc_bias_kernel(tc, x, tab_words, tab_scales, cw, cb, al_wor
 
         tscale = keep.tile([P, T], U8, name="tscale", tag="tscale", align_bytes=64)
         nc.vector.memset(tscale[:].bitcast(I32), 0)
-        ascale = keep.tile([P, PASSES, N], U8, name="ascale", align_bytes=64)
-        nc.vector.memset(ascale[:].rearrange("p a n -> p (a n)").bitcast(I32), 0)
 
         x_rows = x.rearrange("(p i) m -> p i m", i=PACK)
 
-        def load_x(c, tag):
-            m0, w = CHUNKS[c]
-            raw = keep.tile([P, PACK, w], F32, name=f"raw{c}", tag=tag, align_bytes=64)
-            nc.sync.dma_start(raw[:], x_rows[:, :, m0 : m0 + w])
+        def load_x(u, tag):
+            raw = keep.tile([P, PACK, UNIT], F32, name=f"raw{u}", tag=tag, align_bytes=64)
+            nc.sync.dma_start(raw[:], x_rows[:, :, u * UNIT : (u + 1) * UNIT])
             return raw
 
         cw_t = keep.tile([P, PASSES, PACK], F32, name="cw_t")
-        cb_t = keep.tile([P, PASSES, PACK], F32, name="cb_t")
-        b_t = keep.tile([P, N // P], F32, name="b_t")
-        al_t = keep.tile([P, PASSES, 2 * N], U8, name="al_t", align_bytes=64)
+        cb_t = keep.tile([P, PASSES, PACK], F32, name="cb_t", tag="cb")
         nc.sync.dma_start(cw_t[:], cw.rearrange("(a p t) -> p a t", p=P, t=PACK))
         nc.sync.dma_start(cb_t[:], cb.rearrange("(a p t) -> p a t", p=P, t=PACK))
 
         raw_first = load_x(0, "raw")
-        for q in range(4):
-            nc.sync.dma_start(tscale[32 * q : 32 * q + 4, :].bitcast(I32), tab_scales[0, 4 * q : 4 * q + 4, :].bitcast(I32))
+        nc.sync.dma_start(tscale[0:P:8, :].bitcast(I32), tab_scales[0].bitcast(I32))
         table = keep.tile([P, T], I32, name="table", tag="table", align_bytes=64)
         nc.sync.dma_start(table[:], tab_words[0].rearrange("p t i -> p (t i)").bitcast(I32))
-
-        for q in range(4):
-            nc.gpsimd.dma_start(
-                ascale[32 * q : 32 * q + 4, :, :].bitcast(I32),
-                al_scales[:, 4 * q : 4 * q + 4, :].rearrange("a r n -> r a n").bitcast(I32),
-            )
-        with nc.allow_non_contiguous_dma(reason="one bias value a partition"):
-            nc.gpsimd.dma_start(b_t[:], b.rearrange("(c p) -> p c", p=P))
-        nc.gpsimd.dma_start(al_t[:].bitcast(I32), al_words.rearrange("a p n -> p a n").bitcast(I32))
 
         picked_scale = keep.tile([P, J], U8, name="picked_scale", tag="xs0", align_bytes=64)
         nc.vector.tensor_copy(picked_scale[:], tscale[:].indirect(offsets[:]))
@@ -81,33 +67,30 @@ def tile_list_kernl_arc_bias_kernel(tc, x, tab_words, tab_scales, cw, cb, al_wor
             v_scale[:].rearrange("p (a t q) -> p a t q", a=PASSES, t=PACK),
             picked_scale[:].rearrange("p (a q t) -> p a t q", a=PASSES, t=PACK),
         )
+        for r in range(1, 4):
+            nc.scalar.dma_start(v_scale[r:P:32, :].bitcast(I32), v_scale[8 * r : P : 32, :].bitcast(I32))
 
-        x_codes, x_scale = [], []
-
+        x_codes = [keep.tile([P, w], U32, name=f"xc{c}", align_bytes=64) for c, (m0, w) in enumerate(CHUNKS)]
+        x_scale = [keep.tile([P, w], U8, name=f"xs{c}", tag=f"xs{c}", align_bytes=64) for c, (m0, w) in enumerate(CHUNKS)]
         x_grouped = {}
 
-        def cast_x(c, raw, copy, tag):
-            w = CHUNKS[c][1]
-            grouped = keep.tile([P, w, PACK], BF16, name=f"xg{c}", tag=tag, align_bytes=64)
+        def cast_x(u, raw, copy, tag):
+            grouped = keep.tile([P, UNIT, PACK], BF16, name=f"xg{u}", tag=tag, align_bytes=64)
             copy(
                 grouped[:].rearrange("p (c i) t -> p c t i", i=4),
                 raw[:].rearrange("p t (c i) -> p c t i", i=4),
             )
-            x_grouped[c] = grouped
+            x_grouped[u] = grouped
 
-        def quantize_x(c):
-            w = CHUNKS[c][1]
-            grouped = x_grouped[c]
-            codes = keep.tile([P, w], U32, name=f"xc{c}", align_bytes=64)
-            scale = keep.tile([P, w], U8, name=f"xs{c}", tag=f"xs{c}", align_bytes=64)
-            nc.vector.quantize_mx(codes[:].bitcast(FP8X4), scale[:], grouped[:].rearrange("p m t -> p (m t)"))
-            x_codes.append(codes)
-            x_scale.append(scale)
+        def quantize_x(u, c):
+            cols = slice(u * UNIT - CHUNKS[c][0], (u + 1) * UNIT - CHUNKS[c][0])
+            nc.vector.quantize_mx(
+                x_codes[c][:, cols].bitcast(FP8X4), x_scale[c][:, cols], x_grouped[u][:].rearrange("p m t -> p (m t)")
+            )
 
         cast_x(0, raw_first, nc.scalar.copy, "xg0")
-        quantize_x(0)
-        raw_second = load_x(1, "raw")
-        raw_third = load_x(2, "tscale")
+        quantize_x(0, 0)
+        raw = {1: load_x(1, "raw"), 2: load_x(2, "tscale")}
 
         sign = keep.tile([P, PASSES * PACK], F32, name="sign")
         gain = keep.tile([P, PASSES * PACK], F32, name="gain")
@@ -119,6 +102,9 @@ def tile_list_kernl_arc_bias_kernel(tc, x, tab_words, tab_scales, cw, cb, al_wor
         for col in range(PASSES * PACK):
             nc.scalar.activation(shift[:, col : col + 1], cb_f[:, col : col + 1], ACT.Copy, scale=gain[:, col : col + 1])
 
+        b_t = keep.tile([P, N // P], F32, name="b_t", tag="cb")
+        with nc.allow_non_contiguous_dma(reason="one bias value a partition"):
+            nc.sync.dma_start(b_t[:], b.rearrange("(c p) -> p c", p=P))
         v_codes = []
         for a in range(PASSES):
             codes = keep.tile([P, PACK, P], U32, name=f"vc{a}", align_bytes=64)
@@ -128,6 +114,20 @@ def tile_list_kernl_arc_bias_kernel(tc, x, tab_words, tab_scales, cw, cb, al_wor
                 table[:].bitcast(U32).indirect(offsets[:, a * cols : (a + 1) * cols]),
             )
             v_codes.append(codes)
+
+        cast_x(1, raw[1], nc.scalar.copy, "xg0")
+        raw_last = load_x(3, "raw")
+        cast_x(2, raw[2], nc.vector.tensor_copy, "table")
+        al_all = keep.tile([P, PASSES * 3 * N], U8, name="al_all", tag="tscale", align_bytes=64)
+        al_t = al_all[:, 0 : PASSES * 2 * N].rearrange("p (a n) -> p a n", a=PASSES)
+        ascale = al_all[:, PASSES * 2 * N :].rearrange("p (a n) -> p a n", a=PASSES)
+        nc.vector.memset(al_all[:, PASSES * 2 * N :].bitcast(I32), 0)
+        nc.sync.dma_start(al_t.bitcast(I32), al_words.rearrange("a p n -> p a n").bitcast(I32))
+        for q in range(4):
+            nc.sync.dma_start(
+                ascale[32 * q : 32 * q + 4, :, :].bitcast(I32),
+                al_scales[:, 4 * q : 4 * q + 4, :].rearrange("a r n -> r a n").bitcast(I32),
+            )
 
         planes = {}
         h_mx = {}
@@ -200,28 +200,28 @@ def tile_list_kernl_arc_bias_kernel(tc, x, tab_words, tab_scales, cw, cb, al_wor
             first = CHUNKS[c][0] + m0
             nc.sync.dma_start(out.rearrange("(g p) m -> p g m", p=P)[:, :, first : first + w], result[:])
 
+        quantize_x(1, 1)
+        quantize_x(2, 1)
         first_stage(0, 0)
-        cast_x(1, raw_second, nc.vector.tensor_copy, "table")
         first_stage(0, 1)
-        apply_sign(0, 0)
-        quantize_x(1)
-        interleave_h(0, 0, 0, 256)
         first_stage(1, 0)
+        apply_sign(0, 0)
+        interleave_h(0, 0, 0, 256)
         apply_sign(0, 1)
         quantize_h(0, 0, 0, 256)
         interleave_h(0, 1, 0, 256)
-        cast_x(2, raw_third, nc.scalar.copy, "hp0_0")
-        first_stage(1, 1)
-        quantize_x(2)
+        cast_x(3, raw_last, nc.vector.tensor_copy, "hp0_1")
         quantize_h(0, 1, 0, 256)
+        quantize_x(3, 2)
+        first_stage(1, 1)
         apply_sign(1, 0)
-        second_stage(0, 0, 256, False)
         interleave_h(1, 0, 0, 512)
         first_stage(2, 0)
         apply_sign(1, 1)
         quantize_h(1, 0, 0, 512)
         interleave_h(1, 1, 0, 512)
         first_stage(2, 1)
+        second_stage(0, 0, 256, False)
         apply_sign(2, 0)
         quantize_h(1, 1, 0, 512)
         interleave_h(2, 0, 0, 256)

@@ -29,68 +29,35 @@ def tile_list_kernl_arc_bias_kernel(tc, x, tab_words, tab_scales, cw, cb, al_wor
     nc = tc.nc
     with ExitStack() as ctx:
         keep = ctx.enter_context(tc.tile_pool(name="keep", bufs=1))
+        reuse = ctx.enter_context(tc.tile_pool(name="reuse", bufs=1))
+        stage = ctx.enter_context(tc.tile_pool(name="stage", bufs=1))
         psum_d = ctx.enter_context(tc.psum_pool(name="psum_d", bufs=4))
         psum_y = ctx.enter_context(tc.psum_pool(name="psum_y", bufs=4))
 
         offsets = keep.tile([P, J // 16], U16, name="offsets")
         nc.sync.dma_start(offsets[:], offs)
 
-        warm = keep.tile([P, 1], F32, name="warm", tag="table", align_bytes=64)
-        nc.vector.memset(warm[:], 0.0)
-        warm_out = keep.tile([P, 1], F32, name="warm_out")
-        nc.scalar.activation(warm_out[:], warm[:], ACT.Relu)
-
-        tscale = keep.tile([P, T], U8, name="tscale", tag="tscale", align_bytes=64)
-        nc.vector.memset(tscale[:].bitcast(I32), 0)
-
-        x_rows = x.rearrange("(p i) m -> p i m", i=PACK)
-
-        def load_x(u, tag):
-            raw = keep.tile([P, PACK, UNIT], F32, name=f"raw{u}", tag=tag, align_bytes=64)
-            nc.sync.dma_start(raw[:], x_rows[:, :, u * UNIT : (u + 1) * UNIT])
-            return raw
+        tscale = keep.tile([P, T], U8, name="tscale", tag="raw1", align_bytes=64)
+        nc.sync.dma_start(tscale[P - 16 : P, :].bitcast(I32), tab_scales[0].bitcast(I32))
+        nc.vector.memset(tscale[0:96, :].bitcast(I32), 0)
+        nc.vector.memset(tscale[96 : P - 16, :].bitcast(I32), 0)
 
         cw_t = keep.tile([P, PASSES, PACK], F32, name="cw_t")
-        cb_t = keep.tile([P, PASSES, PACK], F32, name="cb_t", tag="cb")
-        nc.sync.dma_start(cw_t[:], cw.rearrange("(a p t) -> p a t", p=P, t=PACK))
-        nc.sync.dma_start(cb_t[:], cb.rearrange("(a p t) -> p a t", p=P, t=PACK))
+        cb_t = keep.tile([P, PASSES, PACK], F32, name="cb_t")
+        nc.scalar.dma_start(cw_t[:], cw.rearrange("(a p t) -> p a t", p=P, t=PACK))
+        nc.scalar.dma_start(cb_t[:], cb.rearrange("(a p t) -> p a t", p=P, t=PACK))
 
-        raw_first = load_x(0, "raw")
-        nc.sync.dma_start(tscale[0:P:8, :].bitcast(I32), tab_scales[0].bitcast(I32))
-        table = keep.tile([P, T], I32, name="table", tag="table", align_bytes=64)
+        table = reuse.tile([P, T], I32, name="table", align_bytes=64, offset=0)
         nc.sync.dma_start(table[:], tab_words[0].rearrange("p t i -> p (t i)").bitcast(I32))
 
-        picked_scale = keep.tile([P, J], U8, name="picked_scale", tag="xs0", align_bytes=64)
-        nc.vector.tensor_copy(picked_scale[:], tscale[:].indirect(offsets[:]))
-        v_scale = keep.tile([P, J], U8, name="v_scale", align_bytes=64)
-        nc.vector.tensor_copy(
-            v_scale[:].rearrange("p (a t q) -> p a t q", a=PASSES, t=PACK),
-            picked_scale[:].rearrange("p (a q t) -> p a t q", a=PASSES, t=PACK),
-        )
-        for r in range(1, 4):
-            nc.scalar.dma_start(v_scale[r:P:32, :].bitcast(I32), v_scale[8 * r : P : 32, :].bitcast(I32))
+        x_rows = x.rearrange("(p i) m -> p i m", i=PACK)
+        raw = {}
 
-        x_codes = [keep.tile([P, w], U32, name=f"xc{c}", align_bytes=64) for c, (m0, w) in enumerate(CHUNKS)]
-        x_scale = [keep.tile([P, w], U8, name=f"xs{c}", tag=f"xs{c}", align_bytes=64) for c, (m0, w) in enumerate(CHUNKS)]
-        x_grouped = {}
+        def load_x(u, pool, **place):
+            raw[u] = pool.tile([P, PACK, UNIT], F32, name=f"raw{u}", align_bytes=64, **place)
+            nc.sync.dma_start(raw[u][:], x_rows[:, :, u * UNIT : (u + 1) * UNIT])
 
-        def cast_x(u, raw, copy, tag):
-            grouped = keep.tile([P, UNIT, PACK], BF16, name=f"xg{u}", tag=tag, align_bytes=64)
-            copy(
-                grouped[:].rearrange("p (c i) t -> p c t i", i=4),
-                raw[:].rearrange("p t (c i) -> p c t i", i=4),
-            )
-            x_grouped[u] = grouped
-
-        def quantize_x(u, c):
-            cols = slice(u * UNIT - CHUNKS[c][0], (u + 1) * UNIT - CHUNKS[c][0])
-            nc.vector.quantize_mx(
-                x_codes[c][:, cols].bitcast(FP8X4), x_scale[c][:, cols], x_grouped[u][:].rearrange("p m t -> p (m t)")
-            )
-
-        cast_x(0, raw_first, nc.scalar.copy, "xg0")
-        quantize_x(0, 0)
-        raw = {1: load_x(1, "raw"), 2: load_x(2, "tscale")}
+        load_x(0, keep)
 
         sign = keep.tile([P, PASSES * PACK], F32, name="sign")
         gain = keep.tile([P, PASSES * PACK], F32, name="gain")
@@ -102,9 +69,18 @@ def tile_list_kernl_arc_bias_kernel(tc, x, tab_words, tab_scales, cw, cb, al_wor
         for col in range(PASSES * PACK):
             nc.scalar.activation(shift[:, col : col + 1], cb_f[:, col : col + 1], ACT.Copy, scale=gain[:, col : col + 1])
 
-        b_t = keep.tile([P, N // P], F32, name="b_t", tag="cb")
-        with nc.allow_non_contiguous_dma(reason="one bias value a partition"):
-            nc.sync.dma_start(b_t[:], b.rearrange("(c p) -> p c", p=P))
+        picked_scale = stage.tile([P, J], U8, name="picked_scale", align_bytes=64, offset=3584)
+        nc.vector.tensor_copy(picked_scale[:], tscale[:].indirect(offsets[:]))
+        v_scale = keep.tile([P, J], U8, name="v_scale", align_bytes=64)
+        nc.vector.tensor_copy(
+            v_scale[:].rearrange("p (a t q) -> p a t q", a=PASSES, t=PACK),
+            picked_scale[:].rearrange("p (a q t) -> p a t q", a=PASSES, t=PACK),
+        )
+        for r in range(4):
+            nc.scalar.dma_start(v_scale[r:P:32, :].bitcast(I32), v_scale[P - 16 + r : P : 4, :].bitcast(I32))
+        load_x(1, keep, tag="raw1")
+        load_x(2, stage, offset=0)
+
         v_codes = []
         for a in range(PASSES):
             codes = keep.tile([P, PACK, P], U32, name=f"vc{a}", align_bytes=64)
@@ -114,15 +90,36 @@ def tile_list_kernl_arc_bias_kernel(tc, x, tab_words, tab_scales, cw, cb, al_wor
                 table[:].bitcast(U32).indirect(offsets[:, a * cols : (a + 1) * cols]),
             )
             v_codes.append(codes)
+        load_x(3, reuse, offset=12288)
 
-        cast_x(1, raw[1], nc.scalar.copy, "xg0")
-        raw_last = load_x(3, "raw")
-        cast_x(2, raw[2], nc.vector.tensor_copy, "table")
-        al_all = keep.tile([P, PASSES * 3 * N], U8, name="al_all", tag="tscale", align_bytes=64)
-        al_t = al_all[:, 0 : PASSES * 2 * N].rearrange("p (a n) -> p a n", a=PASSES)
-        ascale = al_all[:, PASSES * 2 * N :].rearrange("p (a n) -> p a n", a=PASSES)
-        nc.vector.memset(al_all[:, PASSES * 2 * N :].bitcast(I32), 0)
+        x_codes = [
+            reuse.tile([P, w], U32, name=f"xc{c}", align_bytes=64, offset=4 * m0) for c, (m0, w) in enumerate(CHUNKS)
+        ]
+        x_scale = [keep.tile([P, w], U8, name=f"xs{c}", align_bytes=64) for c, (m0, w) in enumerate(CHUNKS)]
+        x_grouped = {}
+
+        def cast_x(u, copy, pool, **place):
+            grouped = pool.tile([P, UNIT, PACK], BF16, name=f"xg{u}", align_bytes=64, **place)
+            copy(
+                grouped[:].rearrange("p (c i) t -> p c t i", i=4),
+                raw[u][:].rearrange("p t (c i) -> p c t i", i=4),
+            )
+            x_grouped[u] = grouped
+
+        def quantize_x(u, c):
+            cols = slice(u * UNIT - CHUNKS[c][0], (u + 1) * UNIT - CHUNKS[c][0])
+            nc.vector.quantize_mx(
+                x_codes[c][:, cols].bitcast(FP8X4), x_scale[c][:, cols], x_grouped[u][:].rearrange("p m t -> p (m t)")
+            )
+
+        late = reuse.tile([P, PASSES * 3 * N], U8, name="late", align_bytes=64, offset=8192)
+        al_t = late[:, 0 : PASSES * 2 * N].rearrange("p (a n) -> p a n", a=PASSES)
+        ascale = late[:, PASSES * 2 * N : PASSES * 3 * N].rearrange("p (a n) -> p a n", a=PASSES)
+        b_t = reuse.tile([P, N // P], F32, name="b_t", align_bytes=64, offset=10240)
+        nc.gpsimd.memset(late[:, PASSES * 2 * N : PASSES * 3 * N].bitcast(I32), 0)
         nc.sync.dma_start(al_t.bitcast(I32), al_words.rearrange("a p n -> p a n").bitcast(I32))
+        with nc.allow_non_contiguous_dma(reason="one bias value a partition"):
+            nc.sync.dma_start(b_t[:], b.rearrange("(c p) -> p c", p=P))
         for q in range(4):
             nc.sync.dma_start(
                 ascale[32 * q : 32 * q + 4, :, :].bitcast(I32),
@@ -200,34 +197,38 @@ def tile_list_kernl_arc_bias_kernel(tc, x, tab_words, tab_scales, cw, cb, al_wor
             first = CHUNKS[c][0] + m0
             nc.sync.dma_start(out.rearrange("(g p) m -> p g m", p=P)[:, :, first : first + w], result[:])
 
-        quantize_x(1, 1)
-        quantize_x(2, 1)
+        cast_x(0, nc.scalar.copy, stage, offset=4096)
+        quantize_x(0, 0)
+        cast_x(1, nc.vector.tensor_copy, reuse, offset=4096)
         first_stage(0, 0)
         first_stage(0, 1)
-        first_stage(1, 0)
+        cast_x(2, nc.vector.tensor_copy, reuse, offset=6144)
+        quantize_x(1, 1)
         apply_sign(0, 0)
+        quantize_x(2, 1)
+        first_stage(1, 0)
         interleave_h(0, 0, 0, 256)
-        apply_sign(0, 1)
+        cast_x(3, nc.vector.tensor_copy, keep, tag="hp0_0")
         quantize_h(0, 0, 0, 256)
-        interleave_h(0, 1, 0, 256)
-        cast_x(3, raw_last, nc.vector.tensor_copy, "hp0_1")
-        quantize_h(0, 1, 0, 256)
+        apply_sign(0, 1)
         quantize_x(3, 2)
         first_stage(1, 1)
-        apply_sign(1, 0)
-        interleave_h(1, 0, 0, 512)
         first_stage(2, 0)
+        first_stage(2, 1)
+        interleave_h(0, 1, 0, 256)
+        apply_sign(1, 0)
+        quantize_h(0, 1, 0, 256)
+        interleave_h(1, 0, 0, 512)
         apply_sign(1, 1)
         quantize_h(1, 0, 0, 512)
         interleave_h(1, 1, 0, 512)
-        first_stage(2, 1)
-        second_stage(0, 0, 256, False)
         apply_sign(2, 0)
         quantize_h(1, 1, 0, 512)
         interleave_h(2, 0, 0, 256)
-        second_stage(1, 0, 512, False)
         apply_sign(2, 1)
         quantize_h(2, 0, 0, 256)
+        second_stage(0, 0, 256, False)
+        second_stage(1, 0, 512, False)
         interleave_h(2, 1, 0, 128)
         interleave_h(2, 1, 128, 128)
         quantize_h(2, 1, 0, 128)

@@ -158,9 +158,9 @@ def tile_list_kernl_arc_bias_kernel(tc, x, tab_words, tab_scales, cw, cb, al_wor
 
         h_grouped = {}
 
-        def interleave_h(c, a, m0, w):
+        def interleave_h(c, a, m0, w, copy=nc.vector.tensor_copy):
             grouped = keep.tile([P, w * PACK], BF16, name=f"hg{c}_{a}_{m0}", align_bytes=64)
-            nc.vector.tensor_copy(
+            copy(
                 grouped[:].rearrange("p (c i t) -> p c t i", i=4, t=PACK),
                 planes[c, a][:, :, m0 : m0 + w].rearrange("p t (c i) -> p c t i", i=4),
             )
@@ -175,6 +175,8 @@ def tile_list_kernl_arc_bias_kernel(tc, x, tab_words, tab_scales, cw, cb, al_wor
         def second_stage(c, m0, w, last):
             step = BANK if w == BANK else P
             result = keep.tile([P, N // P, w], F32, name=f"res{c}_{m0}")
+            first = CHUNKS[c][0] + m0
+            target = out.rearrange("(g p) m -> p g m", p=P)[:, :, first : first + w]
             for g in range(N // P):
                 y = psum_y.tile([P, BANK], F32, name="y")
                 for s0 in range(0, w, step):
@@ -194,8 +196,10 @@ def tile_list_kernl_arc_bias_kernel(tc, x, tab_words, tab_scales, cw, cb, al_wor
                     nc.vector.tensor_scalar(result[:, g, :], y[:, 0:w], b_t[:, g : g + 1], None, ALU.add)
                 else:
                     nc.scalar.activation(result[:, g, :], y[:, 0:w], ACT.Identity, bias=b_t[:, g : g + 1])
-            first = CHUNKS[c][0] + m0
-            nc.sync.dma_start(out.rearrange("(g p) m -> p g m", p=P)[:, :, first : first + w], result[:])
+                if w == BANK:
+                    nc.sync.dma_start(target[:, g, :], result[:, g, :])
+            if w != BANK:
+                nc.sync.dma_start(target, result[:])
 
         cast_x(0, nc.scalar.copy, stage, offset=4096)
         quantize_x(0, 0)
@@ -213,24 +217,24 @@ def tile_list_kernl_arc_bias_kernel(tc, x, tab_words, tab_scales, cw, cb, al_wor
         apply_sign(0, 1)
         quantize_x(3, 2)
         first_stage(1, 1)
-        first_stage(2, 0)
-        first_stage(2, 1)
         interleave_h(0, 1, 0, 256)
         apply_sign(1, 0)
         quantize_h(0, 1, 0, 256)
+        second_stage(0, 0, 256, False)
+        first_stage(2, 0)
+        first_stage(2, 1)
         interleave_h(1, 0, 0, 512)
         apply_sign(1, 1)
         quantize_h(1, 0, 0, 512)
         interleave_h(1, 1, 0, 512)
         apply_sign(2, 0)
+        interleave_h(2, 0, 0, 256, nc.scalar.copy)
         quantize_h(1, 1, 0, 512)
-        interleave_h(2, 0, 0, 256)
-        apply_sign(2, 1)
-        quantize_h(2, 0, 0, 256)
-        second_stage(0, 0, 256, False)
         second_stage(1, 0, 512, False)
+        apply_sign(2, 1)
         interleave_h(2, 1, 0, 128)
         interleave_h(2, 1, 128, 128)
+        quantize_h(2, 0, 0, 256)
         quantize_h(2, 1, 0, 128)
         second_stage(2, 0, 128, False)
         quantize_h(2, 1, 128, 128)

@@ -116,7 +116,7 @@ def tile_list_kernl_arc_bias_kernel(tc, x, tab_words, tab_scales, cw, cb, al_wor
         al_t = late[:, 0 : PASSES * 2 * N].rearrange("p (a n) -> p a n", a=PASSES)
         ascale = late[:, PASSES * 2 * N : PASSES * 3 * N].rearrange("p (a n) -> p a n", a=PASSES)
         b_t = reuse.tile([P, N // P], F32, name="b_t", align_bytes=64, offset=10240)
-        nc.gpsimd.memset(late[:, PASSES * 2 * N : PASSES * 3 * N].bitcast(I32), 0)
+        nc.vector.memset(late[:, PASSES * 2 * N : PASSES * 3 * N].bitcast(I32), 0)
         nc.sync.dma_start(al_t.bitcast(I32), al_words.rearrange("a p n -> p a n").bitcast(I32))
         with nc.allow_non_contiguous_dma(reason="one bias value a partition"):
             nc.sync.dma_start(b_t[:], b.rearrange("(c p) -> p c", p=P))
@@ -131,7 +131,7 @@ def tile_list_kernl_arc_bias_kernel(tc, x, tab_words, tab_scales, cw, cb, al_wor
 
         def first_stage(c, a):
             w = CHUNKS[c][1]
-            plane = keep.tile([P, PACK, w], BF16, name=f"hp{c}_{a}", tag=f"hp{c}_{a}", align_bytes=64)
+            rows = []
             for t in range(PACK):
                 d = psum_d.tile([P, BANK], F32, name="d")
                 col = a * PACK + t
@@ -144,16 +144,16 @@ def tile_list_kernl_arc_bias_kernel(tc, x, tab_words, tab_scales, cw, cb, al_wor
                     start=True,
                     stop=True,
                 )
-                nc.scalar.activation(
-                    plane[:, t, :], d[:, 0:w], ACT.Relu, bias=shift[:, col : col + 1], scale=gain[:, col : col + 1]
-                )
-            planes[c, a] = plane
+                row = keep.tile([P, w], BF16, name=f"row{c}_{a}_{t}", tag=f"row{c}_{a}_{t}", align_bytes=64)
+                nc.scalar.activation(row[:], d[:, 0:w], ACT.Relu, bias=shift[:, col : col + 1], scale=gain[:, col : col + 1])
+                rows.append(row)
+            planes[c, a] = rows
 
         def apply_sign(c, a):
             signed = keep.tile([P, PACK, CHUNKS[c][1]], BF16, name=f"hs{c}_{a}", align_bytes=64)
             for t in range(PACK):
                 col = a * PACK + t
-                nc.vector.tensor_scalar(signed[:, t, :], planes[c, a][:, t, :], sign[:, col : col + 1], None, ALU.mult)
+                nc.vector.tensor_scalar(signed[:, t, :], planes[c, a][t][:], sign[:, col : col + 1], None, ALU.mult)
             planes[c, a] = signed
 
         h_grouped = {}
@@ -166,10 +166,11 @@ def tile_list_kernl_arc_bias_kernel(tc, x, tab_words, tab_scales, cw, cb, al_wor
             )
             h_grouped[c, a, m0] = grouped
 
-        def quantize_h(c, a, m0, w):
-            codes = keep.tile([P, w], U32, name=f"hc{c}_{a}_{m0}", align_bytes=64)
+        def quantize_h(c, a, m0, w, g0=None, slot=None):
+            g0 = m0 if g0 is None else g0
+            codes = keep.tile([P, w], U32, name=f"hc{c}_{a}_{m0}", tag=slot or f"hc{c}_{a}_{m0}", align_bytes=64)
             scale = keep.tile([P, w], U8, name=f"hq{c}_{a}_{m0}", align_bytes=64)
-            nc.vector.quantize_mx(codes[:].bitcast(FP8X4), scale[:], h_grouped[c, a, m0][:])
+            nc.vector.quantize_mx(codes[:].bitcast(FP8X4), scale[:], h_grouped[c, a, g0][:, PACK * (m0 - g0) : PACK * (m0 - g0 + w)])
             h_mx[c, a] = (codes, scale, m0)
 
         def second_stage(c, m0, w, last):
@@ -208,30 +209,32 @@ def tile_list_kernl_arc_bias_kernel(tc, x, tab_words, tab_scales, cw, cb, al_wor
         first_stage(0, 1)
         cast_x(2, nc.vector.tensor_copy, reuse, offset=6144)
         quantize_x(1, 1)
-        apply_sign(0, 0)
         quantize_x(2, 1)
+        apply_sign(0, 0)
         first_stage(1, 0)
+        cast_x(3, nc.vector.tensor_copy, keep, tag="row0_0_0")
         interleave_h(0, 0, 0, 256)
-        cast_x(3, nc.vector.tensor_copy, keep, tag="hp0_0")
-        quantize_h(0, 0, 0, 256)
-        apply_sign(0, 1)
         quantize_x(3, 2)
+        apply_sign(0, 1)
+        quantize_h(0, 0, 0, 256, slot="row0_1_0")
         first_stage(1, 1)
         interleave_h(0, 1, 0, 256)
         apply_sign(1, 0)
-        quantize_h(0, 1, 0, 256)
+        quantize_h(0, 1, 0, 256, slot="row1_0_0")
         second_stage(0, 0, 256, False)
         first_stage(2, 0)
         first_stage(2, 1)
         interleave_h(1, 0, 0, 512)
         apply_sign(1, 1)
-        quantize_h(1, 0, 0, 512)
+        quantize_h(1, 0, 0, 512, slot="row1_1_0")
         interleave_h(1, 1, 0, 512)
         apply_sign(2, 0)
         interleave_h(2, 0, 0, 256, nc.scalar.copy)
-        quantize_h(1, 1, 0, 512)
-        second_stage(1, 0, 512, False)
+        quantize_h(1, 1, 0, 256, slot="row2_0_0")
+        second_stage(1, 0, 256, False)
         apply_sign(2, 1)
+        quantize_h(1, 1, 256, 256, 0, slot="row2_1_0")
+        second_stage(1, 256, 256, False)
         interleave_h(2, 1, 0, 128)
         interleave_h(2, 1, 128, 128)
         quantize_h(2, 0, 0, 256)

@@ -31,13 +31,14 @@ def tile_list_kernl_arc_bias_kernel(tc, x, tab_words, tab_scales, cw, cb, al_wor
         keep = ctx.enter_context(tc.tile_pool(name="keep", bufs=1))
         reuse = ctx.enter_context(tc.tile_pool(name="reuse", bufs=1))
         stage = ctx.enter_context(tc.tile_pool(name="stage", bufs=1))
+        early = ctx.enter_context(tc.tile_pool(name="early", bufs=1))
         psum_d = ctx.enter_context(tc.psum_pool(name="psum_d", bufs=4))
         psum_y = ctx.enter_context(tc.psum_pool(name="psum_y", bufs=4))
 
         offsets = keep.tile([P, J // 16], U16, name="offsets")
         nc.sync.dma_start(offsets[:], offs)
 
-        tscale = keep.tile([P, T], U8, name="tscale", tag="raw1", align_bytes=64)
+        tscale = early.tile([P, T], U8, name="tscale", align_bytes=64, offset=0)
         nc.sync.dma_start(tscale[P - 16 : P, :].bitcast(I32), tab_scales[0].bitcast(I32))
         nc.vector.memset(tscale[0:96, :].bitcast(I32), 0)
         nc.vector.memset(tscale[96 : P - 16, :].bitcast(I32), 0)
@@ -47,9 +48,6 @@ def tile_list_kernl_arc_bias_kernel(tc, x, tab_words, tab_scales, cw, cb, al_wor
         nc.scalar.dma_start(cw_t[:], cw.rearrange("(a p t) -> p a t", p=P, t=PACK))
         nc.scalar.dma_start(cb_t[:], cb.rearrange("(a p t) -> p a t", p=P, t=PACK))
 
-        table = reuse.tile([P, T], I32, name="table", align_bytes=64, offset=0)
-        nc.sync.dma_start(table[:], tab_words[0].rearrange("p t i -> p (t i)").bitcast(I32))
-
         x_rows = x.rearrange("(p i) m -> p i m", i=PACK)
         raw = {}
 
@@ -57,7 +55,9 @@ def tile_list_kernl_arc_bias_kernel(tc, x, tab_words, tab_scales, cw, cb, al_wor
             raw[u] = pool.tile([P, PACK, UNIT], F32, name=f"raw{u}", align_bytes=64, **place)
             nc.sync.dma_start(raw[u][:], x_rows[:, :, u * UNIT : (u + 1) * UNIT])
 
-        load_x(0, keep)
+        load_x(0, keep, tag="raw0")
+        table = reuse.tile([P, T], I32, name="table", align_bytes=64, offset=0)
+        nc.sync.dma_start(table[:], tab_words[0].rearrange("p t i -> p (t i)").bitcast(I32))
 
         sign = keep.tile([P, PASSES * PACK], F32, name="sign")
         gain = keep.tile([P, PASSES * PACK], F32, name="gain")
@@ -78,24 +78,10 @@ def tile_list_kernl_arc_bias_kernel(tc, x, tab_words, tab_scales, cw, cb, al_wor
         )
         for r in range(4):
             nc.scalar.dma_start(v_scale[r:P:32, :].bitcast(I32), v_scale[P - 16 + r : P : 4, :].bitcast(I32))
-        load_x(1, keep, tag="raw1")
-        load_x(2, stage, offset=0)
+        load_x(1, early, offset=0)
 
-        v_codes = []
-        for a in range(PASSES):
-            codes = keep.tile([P, PACK, P], U32, name=f"vc{a}", align_bytes=64)
-            cols = PASS // 16
-            nc.vector.tensor_copy(
-                codes[:].rearrange("p t q -> p q t"),
-                table[:].bitcast(U32).indirect(offsets[:, a * cols : (a + 1) * cols]),
-            )
-            v_codes.append(codes)
-        load_x(3, reuse, offset=12288)
-
-        x_codes = [
-            reuse.tile([P, w], U32, name=f"xc{c}", align_bytes=64, offset=4 * m0) for c, (m0, w) in enumerate(CHUNKS)
-        ]
-        x_scale = [keep.tile([P, w], U8, name=f"xs{c}", align_bytes=64) for c, (m0, w) in enumerate(CHUNKS)]
+        x_codes = [keep.tile([P, w], U32, name=f"xc{c}", align_bytes=64) for c, (m0, w) in enumerate(CHUNKS)]
+        x_scale = {}
         x_grouped = {}
 
         def cast_x(u, copy, pool, **place):
@@ -106,11 +92,28 @@ def tile_list_kernl_arc_bias_kernel(tc, x, tab_words, tab_scales, cw, cb, al_wor
             )
             x_grouped[u] = grouped
 
-        def quantize_x(u, c):
+        def quantize_x(u, c, pool=keep, **place):
+            if c not in x_scale:
+                x_scale[c] = pool.tile([P, CHUNKS[c][1]], U8, name=f"xs{c}", align_bytes=64, **place)
             cols = slice(u * UNIT - CHUNKS[c][0], (u + 1) * UNIT - CHUNKS[c][0])
             nc.vector.quantize_mx(
                 x_codes[c][:, cols].bitcast(FP8X4), x_scale[c][:, cols], x_grouped[u][:].rearrange("p m t -> p (m t)")
             )
+
+        cast_x(0, nc.vector.tensor_copy, stage, offset=4096)
+        load_x(2, keep, tag="raw0")
+        quantize_x(0, 0)
+        load_x(3, stage, offset=1024)
+        v_codes = []
+        for a in range(PASSES):
+            pool, place = (stage, {"offset": 5120}) if a == 0 else (keep, {})
+            codes = pool.tile([P, PACK, P], U32, name=f"vc{a}", align_bytes=64, **place)
+            cols = PASS // 16
+            nc.vector.tensor_copy(
+                codes[:].rearrange("p t q -> p q t"),
+                table[:].bitcast(U32).indirect(offsets[:, a * cols : (a + 1) * cols]),
+            )
+            v_codes.append(codes)
 
         late = reuse.tile([P, PASSES * 3 * N], U8, name="late", align_bytes=64, offset=8192)
         al_t = late[:, 0 : PASSES * 2 * N].rearrange("p (a n) -> p a n", a=PASSES)
@@ -144,7 +147,8 @@ def tile_list_kernl_arc_bias_kernel(tc, x, tab_words, tab_scales, cw, cb, al_wor
                     start=True,
                     stop=True,
                 )
-                row = keep.tile([P, w], BF16, name=f"row{c}_{a}_{t}", tag=f"row{c}_{a}_{t}", align_bytes=64)
+                pool, place = (early, {"offset": 512 * t}) if (c, a) == (0, 0) else (keep, {"tag": f"row{c}_{a}_{t}"})
+                row = pool.tile([P, w], BF16, name=f"row{c}_{a}_{t}", align_bytes=64, **place)
                 nc.scalar.activation(row[:], d[:, 0:w], ACT.Relu, bias=shift[:, col : col + 1], scale=gain[:, col : col + 1])
                 rows.append(row)
             planes[c, a] = rows
@@ -202,19 +206,17 @@ def tile_list_kernl_arc_bias_kernel(tc, x, tab_words, tab_scales, cw, cb, al_wor
             if w != BANK:
                 nc.sync.dma_start(target, result[:])
 
-        cast_x(0, nc.scalar.copy, stage, offset=4096)
-        quantize_x(0, 0)
-        cast_x(1, nc.vector.tensor_copy, reuse, offset=4096)
+        cast_x(1, nc.scalar.copy, keep, tag="xg1")
         first_stage(0, 0)
         first_stage(0, 1)
         cast_x(2, nc.vector.tensor_copy, reuse, offset=6144)
-        quantize_x(1, 1)
+        quantize_x(1, 1, reuse, offset=0)
         quantize_x(2, 1)
+        cast_x(3, nc.vector.tensor_copy, keep, tag="xg1")
         apply_sign(0, 0)
         first_stage(1, 0)
-        cast_x(3, nc.vector.tensor_copy, keep, tag="row0_0_0")
+        quantize_x(3, 2, early, offset=0)
         interleave_h(0, 0, 0, 256)
-        quantize_x(3, 2)
         apply_sign(0, 1)
         quantize_h(0, 0, 0, 256, slot="row0_1_0")
         first_stage(1, 1)

@@ -21,27 +21,35 @@ PACK = 4
 PASS = P * PACK
 PASSES = J // PASS
 BANK = 512
-UNIT = 256
-CHUNKS = [(0, 256), (256, 512), (768, 256)]
+QUADRANT = 32
+SCALE_ROWS = PASS // 32
+LIST_ROWS = 16
+RUN = 4
+FLOAT_MAX = (2.0 - 2.0**-23) * 2.0**127
+QUARTER = M // 4
+CHUNKS = [(0, QUARTER), (QUARTER, 2 * QUARTER), (3 * QUARTER, QUARTER)]
+VECTOR_ROW = (1, 0, PACK - 1)
 
 
 def tile_list_kernl_arc_bias_kernel(tc, x, tab_words, tab_scales, cw, cb, al_words, al_scales, b, offs, out):
     nc = tc.nc
     with ExitStack() as ctx:
         keep = ctx.enter_context(tc.tile_pool(name="keep", bufs=1))
-        reuse = ctx.enter_context(tc.tile_pool(name="reuse", bufs=1))
-        stage = ctx.enter_context(tc.tile_pool(name="stage", bufs=1))
-        early = ctx.enter_context(tc.tile_pool(name="early", bufs=1))
+        on_table = ctx.enter_context(tc.tile_pool(name="on_table", bufs=1))
+        on_picked = ctx.enter_context(tc.tile_pool(name="on_picked", bufs=1))
+        on_scales = ctx.enter_context(tc.tile_pool(name="on_scales", bufs=1))
         psum_d = ctx.enter_context(tc.psum_pool(name="psum_d", bufs=4))
         psum_y = ctx.enter_context(tc.psum_pool(name="psum_y", bufs=4))
 
-        offsets = keep.tile([P, J // 16], U16, name="offsets")
+        offsets = keep.tile([P, J // LIST_ROWS], U16, name="offsets")
         nc.sync.dma_start(offsets[:], offs)
 
-        tscale = early.tile([P, T], U8, name="tscale", align_bytes=64, offset=0)
-        nc.sync.dma_start(tscale[P - 16 : P, :].bitcast(I32), tab_scales[0].bitcast(I32))
-        nc.vector.memset(tscale[0:96, :].bitcast(I32), 0)
-        nc.vector.memset(tscale[96 : P - 16, :].bitcast(I32), 0)
+        first_row = P - SCALE_ROWS
+        last_quadrant = P - QUADRANT
+        table_scales = on_scales.tile([P, T], U8, name="table_scales", align_bytes=64, offset=0)
+        nc.sync.dma_start(table_scales[first_row:P, :].bitcast(I32), tab_scales[0].bitcast(I32))
+        nc.vector.memset(table_scales[0:last_quadrant, :].bitcast(I32), 0)
+        nc.vector.memset(table_scales[last_quadrant:first_row, :].bitcast(I32), 0)
 
         cw_t = keep.tile([P, PASSES, PACK], F32, name="cw_t")
         cb_t = keep.tile([P, PASSES, PACK], F32, name="cb_t")
@@ -52,11 +60,11 @@ def tile_list_kernl_arc_bias_kernel(tc, x, tab_words, tab_scales, cw, cb, al_wor
         raw = {}
 
         def load_x(u, pool, **place):
-            raw[u] = pool.tile([P, PACK, UNIT], F32, name=f"raw{u}", align_bytes=64, **place)
-            nc.sync.dma_start(raw[u][:], x_rows[:, :, u * UNIT : (u + 1) * UNIT])
+            raw[u] = pool.tile([P, PACK, QUARTER], F32, name=f"raw{u}", align_bytes=64, **place)
+            nc.sync.dma_start(raw[u][:], x_rows[:, :, u * QUARTER : (u + 1) * QUARTER])
 
-        load_x(0, keep, tag="raw0")
-        table = reuse.tile([P, T], I32, name="table", align_bytes=64, offset=0)
+        load_x(0, keep, tag="raw_first_third")
+        table = on_table.tile([P, T], I32, name="table", align_bytes=64, offset=0)
         nc.sync.dma_start(table[:], tab_words[0].rearrange("p t i -> p (t i)").bitcast(I32))
 
         sign = keep.tile([P, PASSES * PACK], F32, name="sign")
@@ -69,72 +77,90 @@ def tile_list_kernl_arc_bias_kernel(tc, x, tab_words, tab_scales, cw, cb, al_wor
         for col in range(PASSES * PACK):
             nc.scalar.activation(shift[:, col : col + 1], cb_f[:, col : col + 1], ACT.Copy, scale=gain[:, col : col + 1])
 
-        picked_scale = stage.tile([P, J], U8, name="picked_scale", align_bytes=64, offset=3584)
-        nc.vector.tensor_copy(picked_scale[:], tscale[:].indirect(offsets[:]))
+        signed_shift = keep.tile([P, 1], F32, name="signed_shift")
+        low = keep.tile([P, 1], F32, name="low")
+        high = keep.tile([P, 1], F32, name="high")
+        vcol = slice(VECTOR_ROW[1] * PACK + VECTOR_ROW[2], VECTOR_ROW[1] * PACK + VECTOR_ROW[2] + 1)
+        nc.scalar.activation(signed_shift[:], cb_f[:, vcol], ACT.Copy, scale=cw_f[:, vcol])
+        nc.scalar.activation(high[:], sign[:, vcol], ACT.Relu, scale=FLOAT_MAX)
+        nc.scalar.activation(low[:], sign[:, vcol], ACT.Relu, scale=-FLOAT_MAX)
+        nc.scalar.activation(low[:], low[:], ACT.Copy, scale=-1.0)
+
+        rounded_at = 4096
+        picked_at = rounded_at - 512
+        al_scale_at = rounded_at + 512
+        raw_last_at = al_scale_at - 4 * PACK * QUARTER
+        words_at = al_scale_at + PASSES * N
+
+        picked_scale = on_picked.tile([P, J], U8, name="picked_scale", align_bytes=64, offset=picked_at)
+        nc.vector.tensor_copy(picked_scale[:], table_scales[:].indirect(offsets[:]))
         v_scale = keep.tile([P, J], U8, name="v_scale", align_bytes=64)
         nc.vector.tensor_copy(
             v_scale[:].rearrange("p (a t q) -> p a t q", a=PASSES, t=PACK),
             picked_scale[:].rearrange("p (a q t) -> p a t q", a=PASSES, t=PACK),
         )
         for r in range(4):
-            nc.scalar.dma_start(v_scale[r:P:32, :].bitcast(I32), v_scale[P - 16 + r : P : 4, :].bitcast(I32))
-        load_x(1, early, offset=0)
+            nc.scalar.dma_start(v_scale[r:P:QUADRANT, :].bitcast(I32), v_scale[first_row + r : P : 4, :].bitcast(I32))
+        load_x(1, on_scales, offset=0)
 
-        x_codes = [keep.tile([P, w], U32, name=f"xc{c}", align_bytes=64) for c, (m0, w) in enumerate(CHUNKS)]
+        x_codes = [keep.tile([P, w], U32, name=f"xc{c}", align_bytes=64) for c, (first, w) in enumerate(CHUNKS)]
         x_scale = {}
-        x_grouped = {}
+        x_rounded = {}
 
-        def cast_x(u, copy, pool, **place):
-            grouped = pool.tile([P, UNIT, PACK], BF16, name=f"xg{u}", align_bytes=64, **place)
+        def round_x(u, copy, pool, **place):
+            x_rounded[u] = pool.tile([P, QUARTER, PACK], BF16, name=f"xg{u}", align_bytes=64, **place)
             copy(
-                grouped[:].rearrange("p (c i) t -> p c t i", i=4),
-                raw[u][:].rearrange("p t (c i) -> p c t i", i=4),
+                x_rounded[u][:].rearrange("p (c i) t -> p c t i", i=RUN),
+                raw[u][:].rearrange("p t (c i) -> p c t i", i=RUN),
             )
-            x_grouped[u] = grouped
 
         def quantize_x(u, c, pool=keep, **place):
             if c not in x_scale:
                 x_scale[c] = pool.tile([P, CHUNKS[c][1]], U8, name=f"xs{c}", align_bytes=64, **place)
-            cols = slice(u * UNIT - CHUNKS[c][0], (u + 1) * UNIT - CHUNKS[c][0])
+            cols = slice(u * QUARTER - CHUNKS[c][0], (u + 1) * QUARTER - CHUNKS[c][0])
             nc.vector.quantize_mx(
-                x_codes[c][:, cols].bitcast(FP8X4), x_scale[c][:, cols], x_grouped[u][:].rearrange("p m t -> p (m t)")
+                x_codes[c][:, cols].bitcast(FP8X4), x_scale[c][:, cols], x_rounded[u][:].rearrange("p m t -> p (m t)")
             )
 
-        cast_x(0, nc.vector.tensor_copy, stage, offset=4096)
-        load_x(2, keep, tag="raw0")
+        round_x(0, nc.vector.tensor_copy, on_picked, offset=rounded_at)
+        load_x(2, keep, tag="raw_first_third")
         quantize_x(0, 0)
-        load_x(3, stage, offset=1024)
-        v_codes = []
-        for a in range(PASSES):
-            pool, place = (stage, {"offset": 5120}) if a == 0 else (keep, {})
-            codes = pool.tile([P, PACK, P], U32, name=f"vc{a}", align_bytes=64, **place)
-            cols = PASS // 16
-            nc.vector.tensor_copy(
-                codes[:].rearrange("p t q -> p q t"),
-                table[:].bitcast(U32).indirect(offsets[:, a * cols : (a + 1) * cols]),
-            )
-            v_codes.append(codes)
-
-        late = reuse.tile([P, PASSES * 3 * N], U8, name="late", align_bytes=64, offset=8192)
-        al_t = late[:, 0 : PASSES * 2 * N].rearrange("p (a n) -> p a n", a=PASSES)
-        ascale = late[:, PASSES * 2 * N : PASSES * 3 * N].rearrange("p (a n) -> p a n", a=PASSES)
-        b_t = reuse.tile([P, N // P], F32, name="b_t", align_bytes=64, offset=10240)
-        nc.vector.memset(late[:, PASSES * 2 * N : PASSES * 3 * N].bitcast(I32), 0)
-        nc.sync.dma_start(al_t.bitcast(I32), al_words.rearrange("a p n -> p a n").bitcast(I32))
-        with nc.allow_non_contiguous_dma(reason="one bias value a partition"):
-            nc.sync.dma_start(b_t[:], b.rearrange("(c p) -> p c", p=P))
-        for q in range(4):
+        load_x(3, on_picked, offset=raw_last_at)
+        al_scale = on_picked.tile([P, PASSES, N], U8, name="al_scale", align_bytes=64, offset=al_scale_at)
+        nc.vector.memset(al_scale[:].bitcast(I32), 0)
+        for q in range(P // QUADRANT):
             nc.sync.dma_start(
-                ascale[32 * q : 32 * q + 4, :, :].bitcast(I32),
+                al_scale[QUADRANT * q : QUADRANT * q + 4, :, :].bitcast(I32),
                 al_scales[:, 4 * q : 4 * q + 4, :].rearrange("a r n -> r a n").bitcast(I32),
             )
 
-        planes = {}
-        h_mx = {}
+        v_codes = []
+        list_cols = PASS // LIST_ROWS
+        for a in range(PASSES):
+            pool, place = (on_picked, {"offset": words_at}) if a == 0 else (keep, {})
+            codes = pool.tile([P, PACK, P], U32, name=f"vc{a}", align_bytes=64, **place)
+            nc.vector.tensor_copy(
+                codes[:].rearrange("p t q -> p q t"),
+                table[:].bitcast(U32).indirect(offsets[:, a * list_cols : (a + 1) * list_cols]),
+            )
+            v_codes.append(codes)
 
-        def first_stage(c, a):
+        wide_scale_at, rounded_third_at, al_at, b_at = 0, 6144, 8192, 10240
+        al_t = on_table.tile([P, PASSES, 2 * N], U8, name="al_t", align_bytes=64, offset=al_at)
+        b_t = on_table.tile([P, N // P], F32, name="b_t", align_bytes=64, offset=b_at)
+        nc.sync.dma_start(al_t[:].bitcast(I32), al_words.rearrange("a p n -> p a n").bitcast(I32))
+        with nc.allow_non_contiguous_dma(reason="one bias value a partition"):
+            nc.sync.dma_start(b_t[:], b.rearrange("(c p) -> p c", p=P))
+
+        rows = {}
+        vector_sum = {}
+        signed = {}
+        h_rounded = {}
+        h_mx = {}
+        y_sums = {}
+
+        def first_product(c, a):
             w = CHUNKS[c][1]
-            rows = []
             for t in range(PACK):
                 d = psum_d.tile([P, BANK], F32, name="d")
                 col = a * PACK + t
@@ -147,100 +173,117 @@ def tile_list_kernl_arc_bias_kernel(tc, x, tab_words, tab_scales, cw, cb, al_wor
                     start=True,
                     stop=True,
                 )
-                pool, place = (early, {"offset": 512 * t}) if (c, a) == (0, 0) else (keep, {"tag": f"row{c}_{a}_{t}"})
-                row = pool.tile([P, w], BF16, name=f"row{c}_{a}_{t}", align_bytes=64, **place)
-                nc.scalar.activation(row[:], d[:, 0:w], ACT.Relu, bias=shift[:, col : col + 1], scale=gain[:, col : col + 1])
-                rows.append(row)
-            planes[c, a] = rows
+                pool, place = (on_scales, {"offset": 2 * w * t}) if (c, a) == (0, 0) else (keep, {})
+                rows[c, a, t] = pool.tile([P, w], BF16, name=f"row{c}_{a}_{t}", align_bytes=64, **place)
+                if (c, a, t) == VECTOR_ROW:
+                    vector_sum[c, a, t] = d
+                else:
+                    nc.scalar.activation(
+                        rows[c, a, t][:], d[:, 0:w], ACT.Relu, bias=shift[:, col : col + 1], scale=gain[:, col : col + 1]
+                    )
+
+        def read_vector_row():
+            nc.vector.tensor_scalar(
+                rows[VECTOR_ROW][:], vector_sum[VECTOR_ROW][:], cw_f[:, vcol], signed_shift[:], ALU.mult, ALU.add
+            )
 
         def apply_sign(c, a):
-            signed = keep.tile([P, PACK, CHUNKS[c][1]], BF16, name=f"hs{c}_{a}", align_bytes=64)
+            signed[c, a] = keep.tile([P, PACK, CHUNKS[c][1]], BF16, name=f"hs{c}_{a}", align_bytes=64)
             for t in range(PACK):
                 col = a * PACK + t
-                nc.vector.tensor_scalar(signed[:, t, :], planes[c, a][t][:], sign[:, col : col + 1], None, ALU.mult)
-            planes[c, a] = signed
-
-        h_grouped = {}
+                if (c, a, t) == VECTOR_ROW:
+                    nc.vector.tensor_scalar(signed[c, a][:, t, :], rows[c, a, t][:], low[:], high[:], ALU.max, ALU.min)
+                else:
+                    nc.vector.tensor_scalar(signed[c, a][:, t, :], rows[c, a, t][:], sign[:, col : col + 1], None, ALU.mult)
 
         def interleave_h(c, a, m0, w, copy=nc.vector.tensor_copy):
-            grouped = keep.tile([P, w * PACK], BF16, name=f"hg{c}_{a}_{m0}", align_bytes=64)
+            if (c, a) not in h_rounded:
+                h_rounded[c, a] = keep.tile([P, CHUNKS[c][1] * PACK], BF16, name=f"hg{c}_{a}", align_bytes=64)
             copy(
-                grouped[:].rearrange("p (c i t) -> p c t i", i=4, t=PACK),
-                planes[c, a][:, :, m0 : m0 + w].rearrange("p t (c i) -> p c t i", i=4),
+                h_rounded[c, a][:, PACK * m0 : PACK * (m0 + w)].rearrange("p (c i t) -> p c t i", i=RUN, t=PACK),
+                signed[c, a][:, :, m0 : m0 + w].rearrange("p t (c i) -> p c t i", i=RUN),
             )
-            h_grouped[c, a, m0] = grouped
 
-        def quantize_h(c, a, m0, w, g0=None, slot=None):
-            g0 = m0 if g0 is None else g0
-            codes = keep.tile([P, w], U32, name=f"hc{c}_{a}_{m0}", tag=slot or f"hc{c}_{a}_{m0}", align_bytes=64)
+        def quantize_h(c, a, m0, w):
+            codes = keep.tile([P, w], U32, name=f"hc{c}_{a}_{m0}", align_bytes=64)
             scale = keep.tile([P, w], U8, name=f"hq{c}_{a}_{m0}", align_bytes=64)
-            nc.vector.quantize_mx(codes[:].bitcast(FP8X4), scale[:], h_grouped[c, a, g0][:, PACK * (m0 - g0) : PACK * (m0 - g0 + w)])
+            nc.vector.quantize_mx(codes[:].bitcast(FP8X4), scale[:], h_rounded[c, a][:, PACK * m0 : PACK * (m0 + w)])
             h_mx[c, a] = (codes, scale, m0)
 
-        def second_stage(c, m0, w, last):
-            step = BANK if w == BANK else P
-            result = keep.tile([P, N // P, w], F32, name=f"res{c}_{m0}")
-            first = CHUNKS[c][0] + m0
-            target = out.rearrange("(g p) m -> p g m", p=P)[:, :, first : first + w]
+        def second_product(c, m0, w, pool, tag):
             for g in range(N // P):
-                y = psum_y.tile([P, BANK], F32, name="y")
-                for s0 in range(0, w, step):
+                y = pool.tile([P, BANK], F32, name=tag)
+                for s0 in range(0, w, P):
                     for a in range(PASSES):
                         codes, scale, base = h_mx[c, a]
-                        cols = slice(m0 + s0 - base, m0 + s0 - base + step)
+                        cols = slice(m0 + s0 - base, m0 + s0 - base + P)
                         nc.tensor.matmul_mx(
-                            y[:, s0 : s0 + step],
+                            y[:, s0 : s0 + P],
                             lhsT=al_t[:, a, 2 * P * g : 2 * P * (g + 1)].bitcast(FP4X4),
-                            lhsT_scale=ascale[:, a, P * g : P * (g + 1)],
+                            lhsT_scale=al_scale[:, a, P * g : P * (g + 1)],
                             rhs=codes[:, cols].bitcast(FP8X4),
                             rhs_scale=scale[:, cols],
                             start=(a == 0),
                             stop=(a == PASSES - 1),
                         )
-                if last and g == 1:
+                y_sums[c, m0, g] = y
+
+        def store(c, m0, w, shared):
+            result = keep.tile([P, N // P, w], F32, name=f"res{c}_{m0}")
+            first = CHUNKS[c][0] + m0
+            for g in range(N // P):
+                y = y_sums[c, m0, g]
+                if shared and g == 1:
                     nc.vector.tensor_scalar(result[:, g, :], y[:, 0:w], b_t[:, g : g + 1], None, ALU.add)
                 else:
                     nc.scalar.activation(result[:, g, :], y[:, 0:w], ACT.Identity, bias=b_t[:, g : g + 1])
-                if w == BANK:
-                    nc.sync.dma_start(target[:, g, :], result[:, g, :])
-            if w != BANK:
-                nc.sync.dma_start(target, result[:])
+            nc.sync.dma_start(out.rearrange("(g p) m -> p g m", p=P)[:, :, first : first + w], result[:])
 
-        cast_x(1, nc.scalar.copy, keep, tag="xg1")
-        first_stage(0, 0)
-        first_stage(0, 1)
-        cast_x(2, nc.vector.tensor_copy, reuse, offset=6144)
-        quantize_x(1, 1, reuse, offset=0)
+        round_x(1, nc.scalar.copy, keep, tag="rounded_second_last")
+        first_product(0, 0)
+        first_product(0, 1)
+        round_x(2, nc.vector.tensor_copy, on_table, offset=rounded_third_at)
+        quantize_x(1, 1, on_table, offset=wide_scale_at)
         quantize_x(2, 1)
-        cast_x(3, nc.vector.tensor_copy, keep, tag="xg1")
+        round_x(3, nc.vector.tensor_copy, keep, tag="rounded_second_last")
         apply_sign(0, 0)
-        first_stage(1, 0)
-        quantize_x(3, 2, early, offset=0)
-        interleave_h(0, 0, 0, 256)
+        first_product(1, 0)
+        quantize_x(3, 2, on_scales, offset=0)
+
+        interleave_h(0, 0, 0, QUARTER)
         apply_sign(0, 1)
-        quantize_h(0, 0, 0, 256, slot="row0_1_0")
-        first_stage(1, 1)
-        interleave_h(0, 1, 0, 256)
+        quantize_h(0, 0, 0, QUARTER)
+        interleave_h(0, 1, 0, QUARTER)
+        read_vector_row()
+        first_product(1, 1)
         apply_sign(1, 0)
-        quantize_h(0, 1, 0, 256, slot="row1_0_0")
-        second_stage(0, 0, 256, False)
-        first_stage(2, 0)
-        first_stage(2, 1)
-        interleave_h(1, 0, 0, 512)
+        quantize_h(0, 1, 0, QUARTER)
+        second_product(0, 0, QUARTER, psum_y, "y")
+        store(0, 0, QUARTER, False)
+        first_product(2, 0)
+        first_product(2, 1)
+        interleave_h(1, 0, 0, 2 * QUARTER)
         apply_sign(1, 1)
-        quantize_h(1, 0, 0, 512, slot="row1_1_0")
-        interleave_h(1, 1, 0, 512)
+        quantize_h(1, 0, 0, 2 * QUARTER)
+
+        interleave_h(1, 1, 0, 3 * P)
+        interleave_h(1, 1, 3 * P, P, nc.scalar.copy)
         apply_sign(2, 0)
-        interleave_h(2, 0, 0, 256, nc.scalar.copy)
-        quantize_h(1, 1, 0, 256, slot="row2_0_0")
-        second_stage(1, 0, 256, False)
+        interleave_h(2, 0, 0, P, nc.scalar.copy)
+        quantize_h(1, 1, 0, QUARTER)
+        second_product(1, 0, QUARTER, psum_y, "y")
+        store(1, 0, QUARTER, False)
+        interleave_h(2, 0, P, P)
+        quantize_h(1, 1, QUARTER, QUARTER)
+        second_product(1, QUARTER, QUARTER, psum_y, "y")
+        store(1, QUARTER, QUARTER, False)
+
         apply_sign(2, 1)
-        quantize_h(1, 1, 256, 256, 0, slot="row2_1_0")
-        second_stage(1, 256, 256, False)
-        interleave_h(2, 1, 0, 128)
-        interleave_h(2, 1, 128, 128)
-        quantize_h(2, 0, 0, 256)
-        quantize_h(2, 1, 0, 128)
-        second_stage(2, 0, 128, False)
-        quantize_h(2, 1, 128, 128)
-        second_stage(2, 128, 128, True)
+        quantize_h(2, 0, 0, QUARTER)
+        interleave_h(2, 1, 0, P)
+        interleave_h(2, 1, P, P)
+        for m0 in (0, P):
+            quantize_h(2, 1, m0, P)
+            second_product(2, m0, P, psum_d, "d")
+        for m0 in (0, P):
+            store(2, m0, P, True)

@@ -200,8 +200,8 @@ def tile_list_kernl_arc_bias_kernel(tc, x, tab_words, tab_scales, cw, cb, al_wor
             if (c, a) not in h_rounded:
                 h_rounded[c, a] = keep.tile([P, CHUNKS[c][1] * PACK], BF16, name=f"hg{c}_{a}", align_bytes=64)
             copy(
-                h_rounded[c, a][:, PACK * m0 : PACK * (m0 + w)].rearrange("p (c i t) -> p c t i", i=RUN, t=PACK),
-                signed[c, a][:, :, m0 : m0 + w].rearrange("p t (c i) -> p c t i", i=RUN),
+                h_rounded[c, a][:, PACK * m0 : PACK * (m0 + w)].rearrange("p (c i t) -> p c t i", i=2 * RUN, t=PACK),
+                signed[c, a][:, :, m0 : m0 + w].rearrange("p t (c i) -> p c t i", i=2 * RUN),
             )
 
         def quantize_h(c, a, m0, w):

@@ -25,7 +25,6 @@ QUADRANT = 32
 SCALE_ROWS = PASS // 32
 LIST_ROWS = 16
 RUN = 4
-FLOAT_MAX = (2.0 - 2.0**-23) * 2.0**127
 QUARTER = M // 4
 CHUNKS = [(0, QUARTER), (QUARTER, 2 * QUARTER), (3 * QUARTER, QUARTER)]
 VECTOR_ROW = (1, 0, PACK - 1)
@@ -67,24 +66,20 @@ def tile_list_kernl_arc_bias_kernel(tc, x, tab_words, tab_scales, cw, cb, al_wor
         table = on_table.tile([P, T], I32, name="table", align_bytes=64, offset=0)
         nc.sync.dma_start(table[:], tab_words[0].rearrange("p t i -> p (t i)").bitcast(I32))
 
-        sign = keep.tile([P, PASSES * PACK], F32, name="sign")
+        sign = keep.tile([P, PASSES, PACK], F32, name="sign")
+        relative = keep.tile([P, PASSES, PACK], F32, name="relative")
         gain = keep.tile([P, PASSES * PACK], F32, name="gain")
         shift = keep.tile([P, PASSES * PACK], F32, name="shift")
         cw_f = cw_t[:].rearrange("p a t -> p (a t)")
         cb_f = cb_t[:].rearrange("p a t -> p (a t)")
+        sign_f = sign[:].rearrange("p a t -> p (a t)")
         nc.scalar.activation(gain[:], cw_f, ACT.Abs)
-        nc.scalar.activation(sign[:], cw_f, ACT.Sign)
+        nc.scalar.activation(sign_f, cw_f, ACT.Sign)
+        nc.scalar.activation(sign_f, sign_f, ACT.Sign, bias=0.5)
         for col in range(PASSES * PACK):
             nc.scalar.activation(shift[:, col : col + 1], cb_f[:, col : col + 1], ACT.Copy, scale=gain[:, col : col + 1])
-
-        signed_shift = keep.tile([P, 1], F32, name="signed_shift")
-        low = keep.tile([P, 1], F32, name="low")
-        high = keep.tile([P, 1], F32, name="high")
-        vcol = slice(VECTOR_ROW[1] * PACK + VECTOR_ROW[2], VECTOR_ROW[1] * PACK + VECTOR_ROW[2] + 1)
-        nc.scalar.activation(signed_shift[:], cb_f[:, vcol], ACT.Copy, scale=cw_f[:, vcol])
-        nc.scalar.activation(high[:], sign[:, vcol], ACT.Relu, scale=FLOAT_MAX)
-        nc.scalar.activation(low[:], sign[:, vcol], ACT.Relu, scale=-FLOAT_MAX)
-        nc.scalar.activation(low[:], low[:], ACT.Copy, scale=-1.0)
+        for a in range(PASSES):
+            nc.scalar.activation(relative[:, a, :], sign[:, a, :], ACT.Copy, scale=sign[:, a, 0:1])
 
         rounded_at = 4096
         picked_at = rounded_at - 512
@@ -173,36 +168,41 @@ def tile_list_kernl_arc_bias_kernel(tc, x, tab_words, tab_scales, cw, cb, al_wor
                     start=True,
                     stop=True,
                 )
-                pool, place = (on_scales, {"offset": 2 * w * t}) if (c, a) == (0, 0) else (keep, {})
-                rows[c, a, t] = pool.tile([P, w], BF16, name=f"row{c}_{a}_{t}", align_bytes=64, **place)
+                if t == 0:
+                    pool, place = (on_scales, {"offset": 0}) if (c, a) == (0, 0) else (keep, {})
+                    signed[c, a] = pool.tile([P, PACK, w], BF16, name=f"hs{c}_{a}", align_bytes=64, **place)
+                    row = signed[c, a][:, 0, :]
+                else:
+                    pool, place = (on_scales, {"offset": 2 * w * (PACK - 1 + t)}) if (c, a) == (0, 0) else (keep, {})
+                    rows[c, a, t] = pool.tile([P, w], BF16, name=f"row{c}_{a}_{t}", align_bytes=64, **place)
+                    row = rows[c, a, t][:]
                 if (c, a, t) == VECTOR_ROW:
                     vector_sum[c, a, t] = d
                 else:
-                    nc.scalar.activation(
-                        rows[c, a, t][:], d[:, 0:w], ACT.Relu, bias=shift[:, col : col + 1], scale=gain[:, col : col + 1]
-                    )
+                    nc.scalar.activation(row, d[:, 0:w], ACT.Relu, bias=shift[:, col : col + 1], scale=gain[:, col : col + 1])
 
         def read_vector_row():
+            col = VECTOR_ROW[1] * PACK + VECTOR_ROW[2]
             nc.vector.tensor_scalar(
-                rows[VECTOR_ROW][:], vector_sum[VECTOR_ROW][:], cw_f[:, vcol], signed_shift[:], ALU.mult, ALU.add
+                rows[VECTOR_ROW][:], vector_sum[VECTOR_ROW][:], gain[:, col : col + 1], shift[:, col : col + 1], ALU.mult, ALU.add
             )
 
         def apply_sign(c, a):
-            signed[c, a] = keep.tile([P, PACK, CHUNKS[c][1]], BF16, name=f"hs{c}_{a}", align_bytes=64)
-            for t in range(PACK):
-                col = a * PACK + t
+            for t in range(1, PACK):
                 if (c, a, t) == VECTOR_ROW:
-                    nc.vector.tensor_scalar(signed[c, a][:, t, :], rows[c, a, t][:], low[:], high[:], ALU.max, ALU.min)
+                    nc.vector.tensor_scalar(signed[c, a][:, t, :], rows[c, a, t][:], 0.0, relative[:, a, t : t + 1], ALU.max, ALU.mult)
                 else:
-                    nc.vector.tensor_scalar(signed[c, a][:, t, :], rows[c, a, t][:], sign[:, col : col + 1], None, ALU.mult)
+                    nc.vector.tensor_scalar(signed[c, a][:, t, :], rows[c, a, t][:], relative[:, a, t : t + 1], None, ALU.mult)
 
-        def interleave_h(c, a, m0, w, copy=nc.vector.tensor_copy):
+        def interleave_h(c, a, m0, w, on_scalar=False):
             if (c, a) not in h_rounded:
                 h_rounded[c, a] = keep.tile([P, CHUNKS[c][1] * PACK], BF16, name=f"hg{c}_{a}", align_bytes=64)
-            copy(
-                h_rounded[c, a][:, PACK * m0 : PACK * (m0 + w)].rearrange("p (c i t) -> p c t i", i=2 * RUN, t=PACK),
-                signed[c, a][:, :, m0 : m0 + w].rearrange("p t (c i) -> p c t i", i=2 * RUN),
-            )
+            woven = h_rounded[c, a][:, PACK * m0 : PACK * (m0 + w)].rearrange("p (c i t) -> p c t i", i=2 * RUN, t=PACK)
+            apart = signed[c, a][:, :, m0 : m0 + w].rearrange("p t (c i) -> p c t i", i=2 * RUN)
+            if on_scalar:
+                nc.scalar.activation(woven, apart, ACT.Copy, scale=sign[:, a, 0:1])
+            else:
+                nc.vector.tensor_scalar(woven, apart, sign[:, a, 0:1], None, ALU.mult)
 
         def quantize_h(c, a, m0, w):
             codes = keep.tile([P, w], U32, name=f"hc{c}_{a}_{m0}", align_bytes=64)
@@ -248,7 +248,7 @@ def tile_list_kernl_arc_bias_kernel(tc, x, tab_words, tab_scales, cw, cb, al_wor
         round_x(3, nc.vector.tensor_copy, keep, tag="rounded_second_last")
         apply_sign(0, 0)
         first_product(1, 0)
-        quantize_x(3, 2, on_scales, offset=0)
+        quantize_x(3, 2, on_scales, offset=2 * QUARTER * PACK)
 
         interleave_h(0, 0, 0, QUARTER)
         apply_sign(0, 1)
@@ -266,10 +266,9 @@ def tile_list_kernl_arc_bias_kernel(tc, x, tab_words, tab_scales, cw, cb, al_wor
         apply_sign(1, 1)
         quantize_h(1, 0, 0, 2 * QUARTER)
 
-        interleave_h(1, 1, 0, 3 * P)
-        interleave_h(1, 1, 3 * P, P, nc.scalar.copy)
+        interleave_h(1, 1, 0, 2 * QUARTER)
         apply_sign(2, 0)
-        interleave_h(2, 0, 0, P, nc.scalar.copy)
+        interleave_h(2, 0, 0, P, True)
         quantize_h(1, 1, 0, QUARTER)
         second_product(1, 0, QUARTER, psum_y, "y")
         store(1, 0, QUARTER, False)

@@ -27,7 +27,7 @@ LIST_ROWS = 16
 RUN = 4
 QUARTER = M // 4
 CHUNKS = [(0, QUARTER), (QUARTER, 2 * QUARTER), (3 * QUARTER, QUARTER)]
-VECTOR_ROW = (1, 0, PACK - 1)
+VECTOR_ROWS = [(1, 0, PACK - 1), (1, 1, PACK - 1)]
 
 
 def tile_list_kernl_arc_bias_kernel(tc, x, tab_words, tab_scales, cw, cb, al_words, al_scales, b, offs, out):
@@ -176,20 +176,20 @@ def tile_list_kernl_arc_bias_kernel(tc, x, tab_words, tab_scales, cw, cb, al_wor
                     pool, place = (on_scales, {"offset": 2 * w * (PACK - 1 + t)}) if (c, a) == (0, 0) else (keep, {})
                     rows[c, a, t] = pool.tile([P, w], BF16, name=f"row{c}_{a}_{t}", align_bytes=64, **place)
                     row = rows[c, a, t][:]
-                if (c, a, t) == VECTOR_ROW:
+                if (c, a, t) in VECTOR_ROWS:
                     vector_sum[c, a, t] = d
                 else:
                     nc.scalar.activation(row, d[:, 0:w], ACT.Relu, bias=shift[:, col : col + 1], scale=gain[:, col : col + 1])
 
-        def read_vector_row():
-            col = VECTOR_ROW[1] * PACK + VECTOR_ROW[2]
+        def read_vector_row(c, a, t):
+            col = a * PACK + t
             nc.vector.tensor_scalar(
-                rows[VECTOR_ROW][:], vector_sum[VECTOR_ROW][:], gain[:, col : col + 1], shift[:, col : col + 1], ALU.mult, ALU.add
+                rows[c, a, t][:], vector_sum[c, a, t][:, 0 : CHUNKS[c][1]], gain[:, col : col + 1], shift[:, col : col + 1], ALU.mult, ALU.add
             )
 
         def apply_sign(c, a):
             for t in range(1, PACK):
-                if (c, a, t) == VECTOR_ROW:
+                if (c, a, t) in VECTOR_ROWS:
                     nc.vector.tensor_scalar(signed[c, a][:, t, :], rows[c, a, t][:], 0.0, relative[:, a, t : t + 1], ALU.max, ALU.mult)
                 else:
                     nc.vector.tensor_scalar(signed[c, a][:, t, :], rows[c, a, t][:], relative[:, a, t : t + 1], None, ALU.mult)
@@ -254,19 +254,21 @@ def tile_list_kernl_arc_bias_kernel(tc, x, tab_words, tab_scales, cw, cb, al_wor
         apply_sign(0, 1)
         quantize_h(0, 0, 0, QUARTER)
         interleave_h(0, 1, 0, QUARTER)
-        read_vector_row()
+        read_vector_row(*VECTOR_ROWS[0])
         first_product(1, 1)
         apply_sign(1, 0)
         quantize_h(0, 1, 0, QUARTER)
         second_product(0, 0, QUARTER, psum_y, "y")
         store(0, 0, QUARTER, False)
+        interleave_h(1, 0, 0, 2 * QUARTER)
+        read_vector_row(*VECTOR_ROWS[1])
         first_product(2, 0)
         first_product(2, 1)
-        interleave_h(1, 0, 0, 2 * QUARTER)
         apply_sign(1, 1)
         quantize_h(1, 0, 0, 2 * QUARTER)
 
-        interleave_h(1, 1, 0, 2 * QUARTER)
+        interleave_h(1, 1, 0, 3 * P)
+        interleave_h(1, 1, 3 * P, P, True)
         apply_sign(2, 0)
         interleave_h(2, 0, 0, P, True)
         quantize_h(1, 1, 0, QUARTER)

@@ -27,7 +27,7 @@ LIST_ROWS = 16
 RUN = 4
 QUARTER = M // 4
 CHUNKS = [(0, QUARTER), (QUARTER, 2 * QUARTER), (3 * QUARTER, QUARTER)]
-VECTOR_ROWS = [(1, 0, PACK - 1), (1, 1, PACK - 1)]
+VECTOR_ROWS = [(1, 0, PACK - 1), (2, 0, PACK - 1)]
 
 
 def tile_list_kernl_arc_bias_kernel(tc, x, tab_words, tab_scales, cw, cb, al_words, al_scales, b, offs, out):
@@ -156,7 +156,9 @@ def tile_list_kernl_arc_bias_kernel(tc, x, tab_words, tab_scales, cw, cb, al_wor
 
         def first_product(c, a):
             w = CHUNKS[c][1]
-            for t in range(PACK):
+            pool, place = (on_scales, {"offset": 0}) if (c, a) == (0, 0) else (keep, {})
+            signed[c, a] = pool.tile([P, PACK, w], BF16, name=f"hs{c}_{a}", align_bytes=64, **place)
+            for t in sorted(range(PACK), key=lambda t: ((c, a, t) in VECTOR_ROWS, t == 0)):
                 d = psum_d.tile([P, BANK], F32, name="d")
                 col = a * PACK + t
                 nc.tensor.matmul_mx(
@@ -169,8 +171,6 @@ def tile_list_kernl_arc_bias_kernel(tc, x, tab_words, tab_scales, cw, cb, al_wor
                     stop=True,
                 )
                 if t == 0:
-                    pool, place = (on_scales, {"offset": 0}) if (c, a) == (0, 0) else (keep, {})
-                    signed[c, a] = pool.tile([P, PACK, w], BF16, name=f"hs{c}_{a}", align_bytes=64, **place)
                     row = signed[c, a][:, 0, :]
                 else:
                     pool, place = (on_scales, {"offset": 2 * w * (PACK - 1 + t)}) if (c, a) == (0, 0) else (keep, {})
@@ -261,11 +261,11 @@ def tile_list_kernl_arc_bias_kernel(tc, x, tab_words, tab_scales, cw, cb, al_wor
         second_product(0, 0, QUARTER, psum_y, "y")
         store(0, 0, QUARTER, False)
         interleave_h(1, 0, 0, 2 * QUARTER)
-        read_vector_row(*VECTOR_ROWS[1])
         first_product(2, 0)
-        first_product(2, 1)
         apply_sign(1, 1)
         quantize_h(1, 0, 0, 2 * QUARTER)
+        read_vector_row(*VECTOR_ROWS[1])
+        first_product(2, 1)
 
         interleave_h(1, 1, 0, 3 * P)
         interleave_h(1, 1, 3 * P, P, True)

@@ -239,7 +239,12 @@ def tile_list_kernl_arc_bias_kernel(tc, x, tab_words, tab_scales, cw, cb, al_wor
                     nc.scalar.activation(result[:, g, :], y[:, 0:w], ACT.Identity, bias=b_t[:, g : g + 1])
             nc.sync.dma_start(out.rearrange("(g p) m -> p g m", p=P)[:, :, first : first + w], result[:])
 
-        round_x(1, nc.scalar.copy, keep, tag="rounded_second_last")
+        x_rounded[1] = keep.tile([P, QUARTER, PACK], BF16, name="xg1", tag="rounded_second_last", align_bytes=64)
+        nc.scalar.copy(
+            x_rounded[1][:, 0:P, :].rearrange("p (c i) t -> p c t i", i=RUN),
+            raw[1][:, :, 0:P].rearrange("p t (c i) -> p c t i", i=RUN),
+        )
+        nc.gpsimd.tensor_scalar(x_rounded[1][:, P:, :], raw[1][:, :, P:].rearrange("p t m -> p m t"), 1.0, 0.0, ALU.mult, ALU.add)
         first_product(0, 0)
         first_product(0, 1)
         round_x(2, nc.vector.tensor_copy, on_table, offset=rounded_third_at)

@@ -27,7 +27,8 @@ LIST_ROWS = 16
 RUN = 4
 QUARTER = M // 4
 CHUNKS = [(0, QUARTER), (QUARTER, 2 * QUARTER), (3 * QUARTER, QUARTER)]
-VECTOR_ROWS = [(1, 0, PACK - 1), (2, 0, PACK - 1)]
+VECTOR_ROWS = [(1, 0, PACK - 2), (1, 0, PACK - 1)]
+GPSIMD_COLUMNS = 192
 
 
 def tile_list_kernl_arc_bias_kernel(tc, x, tab_words, tab_scales, cw, cb, al_words, al_scales, b, offs, out):
@@ -194,12 +195,21 @@ def tile_list_kernl_arc_bias_kernel(tc, x, tab_words, tab_scales, cw, cb, al_wor
                 else:
                     nc.vector.tensor_scalar(signed[c, a][:, t, :], rows[c, a, t][:], relative[:, a, t : t + 1], None, ALU.mult)
 
-        def interleave_h(c, a, m0, w, on_scalar=False):
+        def interleave_h(c, a, m0, w, on_scalar=False, on_gpsimd=False):
             if (c, a) not in h_rounded:
                 h_rounded[c, a] = keep.tile([P, CHUNKS[c][1] * PACK], BF16, name=f"hg{c}_{a}", align_bytes=64)
             woven = h_rounded[c, a][:, PACK * m0 : PACK * (m0 + w)].rearrange("p (c i t) -> p c t i", i=2 * RUN, t=PACK)
             apart = signed[c, a][:, :, m0 : m0 + w].rearrange("p t (c i) -> p c t i", i=2 * RUN)
-            if on_scalar:
+            if on_gpsimd:
+                nc.gpsimd.tensor_scalar(
+                    h_rounded[c, a][:, PACK * m0 : PACK * (m0 + w)].rearrange("p (m t) -> p m t", t=PACK),
+                    signed[c, a][:, :, m0 : m0 + w].rearrange("p t m -> p m t"),
+                    sign[:, a, 0:1],
+                    0.0,
+                    ALU.mult,
+                    ALU.add,
+                )
+            elif on_scalar:
                 nc.scalar.activation(woven, apart, ACT.Copy, scale=sign[:, a, 0:1])
             else:
                 nc.vector.tensor_scalar(woven, apart, sign[:, a, 0:1], None, ALU.mult)
@@ -258,8 +268,10 @@ def tile_list_kernl_arc_bias_kernel(tc, x, tab_words, tab_scales, cw, cb, al_wor
         interleave_h(0, 0, 0, QUARTER)
         apply_sign(0, 1)
         quantize_h(0, 0, 0, QUARTER)
-        interleave_h(0, 1, 0, QUARTER)
+        interleave_h(0, 1, 0, GPSIMD_COLUMNS, on_gpsimd=True)
         read_vector_row(*VECTOR_ROWS[0])
+        read_vector_row(*VECTOR_ROWS[1])
+        interleave_h(0, 1, GPSIMD_COLUMNS, QUARTER - GPSIMD_COLUMNS)
         first_product(1, 1)
         apply_sign(1, 0)
         quantize_h(0, 1, 0, QUARTER)
@@ -269,7 +281,6 @@ def tile_list_kernl_arc_bias_kernel(tc, x, tab_words, tab_scales, cw, cb, al_wor
         first_product(2, 0)
         apply_sign(1, 1)
         quantize_h(1, 0, 0, 2 * QUARTER)
-        read_vector_row(*VECTOR_ROWS[1])
         first_product(2, 1)
 
         interleave_h(1, 1, 0, 3 * P)

@@ -291,14 +291,14 @@ def tile_list_kernl_arc_bias_kernel(tc, x, tab_words, tab_scales, cw, cb, al_wor
         second_product(1, 0, QUARTER, psum_y, "y")
         store(1, 0, QUARTER, False)
         interleave_h(2, 0, P, P)
+        apply_sign(2, 1)
+        interleave_h(2, 1, 0, P)
         quantize_h(1, 1, QUARTER, QUARTER)
         second_product(1, QUARTER, QUARTER, psum_y, "y")
         store(1, QUARTER, QUARTER, False)
 
-        apply_sign(2, 1)
-        quantize_h(2, 0, 0, QUARTER)
-        interleave_h(2, 1, 0, P)
         interleave_h(2, 1, P, P)
+        quantize_h(2, 0, 0, QUARTER)
         for m0 in (0, P):
             quantize_h(2, 1, m0, P)
             second_product(2, m0, P, psum_d, "d")

from contextlib import ExitStack

import concourse.mybir as mybir

K, M, N, J, T = 512, 1024, 256, 1024, 4096
FLOPS = 2 * K * J * M + 2 * J * N * M

F32 = mybir.dt.float32
BF16 = mybir.dt.bfloat16
I32 = mybir.dt.int32
U32 = mybir.dt.uint32
U16 = mybir.dt.uint16
U8 = mybir.dt.uint8
FP8X4 = mybir.dt.float8_e4m3fn_x4
FP4X4 = mybir.dt.float4_e2m1fn_x4
ALU = mybir.AluOpType
ACT = mybir.ActivationFunctionType

P = 128
PACK = 4
PASS = P * PACK
PASSES = J // PASS
BANK = 512
QUADRANT = 32
SCALE_ROWS = PASS // 32
LIST_ROWS = 16
RUN = 4
QUARTER = M // 4
CHUNKS = [(0, QUARTER), (QUARTER, 2 * QUARTER), (3 * QUARTER, QUARTER)]
VECTOR_ROWS = [(1, 0, PACK - 2), (1, 0, PACK - 1)]
GPSIMD_COLUMNS = 192


def tile_list_kernl_arc_bias_kernel(tc, x, tab_words, tab_scales, cw, cb, al_words, al_scales, b, offs, out):
    nc = tc.nc
    with ExitStack() as ctx:
        keep = ctx.enter_context(tc.tile_pool(name="keep", bufs=1))
        on_table = ctx.enter_context(tc.tile_pool(name="on_table", bufs=1))
        on_picked = ctx.enter_context(tc.tile_pool(name="on_picked", bufs=1))
        on_scales = ctx.enter_context(tc.tile_pool(name="on_scales", bufs=1))
        psum_d = ctx.enter_context(tc.psum_pool(name="psum_d", bufs=4))
        psum_y = ctx.enter_context(tc.psum_pool(name="psum_y", bufs=4))

        offsets = keep.tile([P, J // LIST_ROWS], U16, name="offsets")
        nc.sync.dma_start(offsets[:], offs)

        first_row = P - SCALE_ROWS
        last_quadrant = P - QUADRANT
        table_scales = on_scales.tile([P, T], U8, name="table_scales", align_bytes=64, offset=0)
        nc.sync.dma_start(table_scales[first_row:P, :].bitcast(I32), tab_scales[0].bitcast(I32))
        nc.vector.memset(table_scales[0:last_quadrant, :].bitcast(I32), 0)
        nc.vector.memset(table_scales[last_quadrant:first_row, :].bitcast(I32), 0)

        cw_t = keep.tile([P, PASSES, PACK], F32, name="cw_t")
        cb_t = keep.tile([P, PASSES, PACK], F32, name="cb_t")
        nc.scalar.dma_start(cw_t[:], cw.rearrange("(a p t) -> p a t", p=P, t=PACK))
        nc.scalar.dma_start(cb_t[:], cb.rearrange("(a p t) -> p a t", p=P, t=PACK))

        x_rows = x.rearrange("(p i) m -> p i m", i=PACK)
        raw = {}

        def load_x(u, pool, **place):
            raw[u] = pool.tile([P, PACK, QUARTER], F32, name=f"raw{u}", align_bytes=64, **place)
            nc.sync.dma_start(raw[u][:], x_rows[:, :, u * QUARTER : (u + 1) * QUARTER])

        load_x(0, keep, tag="raw_first_third")
        table = on_table.tile([P, T], I32, name="table", align_bytes=64, offset=0)
        nc.sync.dma_start(table[:], tab_words[0].rearrange("p t i -> p (t i)").bitcast(I32))

        sign = keep.tile([P, PASSES, PACK], F32, name="sign")
        relative = keep.tile([P, PASSES, PACK], F32, name="relative")
        gain = keep.tile([P, PASSES * PACK], F32, name="gain")
        shift = keep.tile([P, PASSES * PACK], F32, name="shift")
        cw_f = cw_t[:].rearrange("p a t -> p (a t)")
        cb_f = cb_t[:].rearrange("p a t -> p (a t)")
        sign_f = sign[:].rearrange("p a t -> p (a t)")
        nc.scalar.activation(gain[:], cw_f, ACT.Abs)
        nc.scalar.activation(sign_f, cw_f, ACT.Sign)
        nc.scalar.activation(sign_f, sign_f, ACT.Sign, bias=0.5)
        for col in range(PASSES * PACK):
            nc.scalar.activation(shift[:, col : col + 1], cb_f[:, col : col + 1], ACT.Copy, scale=gain[:, col : col + 1])
        for a in range(PASSES):
            nc.scalar.activation(relative[:, a, :], sign[:, a, :], ACT.Copy, scale=sign[:, a, 0:1])

        rounded_at = 4096
        picked_at = rounded_at - 512
        al_scale_at = rounded_at + 512
        raw_last_at = al_scale_at - 4 * PACK * QUARTER
        words_at = al_scale_at + PASSES * N

        picked_scale = on_picked.tile([P, J], U8, name="picked_scale", align_bytes=64, offset=picked_at)
        nc.vector.tensor_copy(picked_scale[:], table_scales[:].indirect(offsets[:]))
        v_scale = keep.tile([P, J], U8, name="v_scale", align_bytes=64)
        nc.vector.tensor_copy(
            v_scale[:].rearrange("p (a t q) -> p a t q", a=PASSES, t=PACK),
            picked_scale[:].rearrange("p (a q t) -> p a t q", a=PASSES, t=PACK),
        )
        for r in range(4):
            nc.scalar.dma_start(v_scale[r:P:QUADRANT, :].bitcast(I32), v_scale[first_row + r : P : 4, :].bitcast(I32))
        load_x(1, on_scales, offset=0)

        x_codes = [keep.tile([P, w], U32, name=f"xc{c}", align_bytes=64) for c, (first, w) in enumerate(CHUNKS)]
        x_scale = {}
        x_rounded = {}

        def round_x(u, copy, pool, **place):
            x_rounded[u] = pool.tile([P, QUARTER, PACK], BF16, name=f"xg{u}", align_bytes=64, **place)
            copy(
                x_rounded[u][:].rearrange("p (c i) t -> p c t i", i=RUN),
                raw[u][:].rearrange("p t (c i) -> p c t i", i=RUN),
            )

        def quantize_x(u, c, pool=keep, **place):
            if c not in x_scale:
                x_scale[c] = pool.tile([P, CHUNKS[c][1]], U8, name=f"xs{c}", align_bytes=64, **place)
            cols = slice(u * QUARTER - CHUNKS[c][0], (u + 1) * QUARTER - CHUNKS[c][0])
            nc.vector.quantize_mx(
                x_codes[c][:, cols].bitcast(FP8X4), x_scale[c][:, cols], x_rounded[u][:].rearrange("p m t -> p (m t)")
            )

        round_x(0, nc.vector.tensor_copy, on_picked, offset=rounded_at)
        load_x(2, keep, tag="raw_first_third")
        quantize_x(0, 0)
        load_x(3, on_picked, offset=raw_last_at)
        al_scale = on_picked.tile([P, PASSES, N], U8, name="al_scale", align_bytes=64, offset=al_scale_at)
        nc.vector.memset(al_scale[:].bitcast(I32), 0)
        for q in range(P // QUADRANT):
            nc.sync.dma_start(
                al_scale[QUADRANT * q : QUADRANT * q + 4, :, :].bitcast(I32),
                al_scales[:, 4 * q : 4 * q + 4, :].rearrange("a r n -> r a n").bitcast(I32),
            )

        v_codes = []
        list_cols = PASS // LIST_ROWS
        for a in range(PASSES):
            pool, place = (on_picked, {"offset": words_at}) if a == 0 else (keep, {})
            codes = pool.tile([P, PACK, P], U32, name=f"vc{a}", align_bytes=64, **place)
            nc.vector.tensor_copy(
                codes[:].rearrange("p t q -> p q t"),
                table[:].bitcast(U32).indirect(offsets[:, a * list_cols : (a + 1) * list_cols]),
            )
            v_codes.append(codes)

        wide_scale_at, rounded_third_at, al_at, b_at = 0, 6144, 8192, 10240
        al_t = on_table.tile([P, PASSES, 2 * N], U8, name="al_t", align_bytes=64, offset=al_at)
        b_t = on_table.tile([P, N // P], F32, name="b_t", align_bytes=64, offset=b_at)
        nc.sync.dma_start(al_t[:].bitcast(I32), al_words.rearrange("a p n -> p a n").bitcast(I32))
        with nc.allow_non_contiguous_dma(reason="one bias value a partition"):
            nc.sync.dma_start(b_t[:], b.rearrange("(c p) -> p c", p=P))

        rows = {}
        vector_sum = {}
        signed = {}
        h_rounded = {}
        h_mx = {}
        y_sums = {}

        def first_product(c, a):
            w = CHUNKS[c][1]
            pool, place = (on_scales, {"offset": 0}) if (c, a) == (0, 0) else (keep, {})
            signed[c, a] = pool.tile([P, PACK, w], BF16, name=f"hs{c}_{a}", align_bytes=64, **place)
            for t in sorted(range(PACK), key=lambda t: ((c, a, t) in VECTOR_ROWS, t == 0)):
                d = psum_d.tile([P, BANK], F32, name="d")
                col = a * PACK + t
                nc.tensor.matmul_mx(
                    d[:, 0:w],
                    lhsT=v_codes[a][:, t, :].bitcast(FP8X4),
                    lhsT_scale=v_scale[:, col * P : (col + 1) * P],
                    rhs=x_codes[c][:].bitcast(FP8X4),
                    rhs_scale=x_scale[c][:],
                    start=True,
                    stop=True,
                )
                if t == 0:
                    row = signed[c, a][:, 0, :]
                else:
                    pool, place = (on_scales, {"offset": 2 * w * (PACK - 1 + t)}) if (c, a) == (0, 0) else (keep, {})
                    rows[c, a, t] = pool.tile([P, w], BF16, name=f"row{c}_{a}_{t}", align_bytes=64, **place)
                    row = rows[c, a, t][:]
                if (c, a, t) in VECTOR_ROWS:
                    vector_sum[c, a, t] = d
                else:
                    nc.scalar.activation(row, d[:, 0:w], ACT.Relu, bias=shift[:, col : col + 1], scale=gain[:, col : col + 1])

        def read_vector_row(c, a, t):
            col = a * PACK + t
            nc.vector.tensor_scalar(
                rows[c, a, t][:], vector_sum[c, a, t][:, 0 : CHUNKS[c][1]], gain[:, col : col + 1], shift[:, col : col + 1], ALU.mult, ALU.add
            )

        def apply_sign(c, a):
            for t in range(1, PACK):
                if (c, a, t) in VECTOR_ROWS:
                    nc.vector.tensor_scalar(signed[c, a][:, t, :], rows[c, a, t][:], 0.0, relative[:, a, t : t + 1], ALU.max, ALU.mult)
                else:
                    nc.vector.tensor_scalar(signed[c, a][:, t, :], rows[c, a, t][:], relative[:, a, t : t + 1], None, ALU.mult)

        def interleave_h(c, a, m0, w, on_scalar=False, on_gpsimd=False):
            if (c, a) not in h_rounded:
                h_rounded[c, a] = keep.tile([P, CHUNKS[c][1] * PACK], BF16, name=f"hg{c}_{a}", align_bytes=64)
            woven = h_rounded[c, a][:, PACK * m0 : PACK * (m0 + w)].rearrange("p (c i t) -> p c t i", i=2 * RUN, t=PACK)
            apart = signed[c, a][:, :, m0 : m0 + w].rearrange("p t (c i) -> p c t i", i=2 * RUN)
            if on_gpsimd:
                nc.gpsimd.tensor_scalar(
                    h_rounded[c, a][:, PACK * m0 : PACK * (m0 + w)].rearrange("p (m t) -> p m t", t=PACK),
                    signed[c, a][:, :, m0 : m0 + w].rearrange("p t m -> p m t"),
                    sign[:, a, 0:1],
                    0.0,
                    ALU.mult,
                    ALU.add,
                )
            elif on_scalar:
                nc.scalar.activation(woven, apart, ACT.Copy, scale=sign[:, a, 0:1])
            else:
                nc.vector.tensor_scalar(woven, apart, sign[:, a, 0:1], None, ALU.mult)

        def quantize_h(c, a, m0, w):
            codes = keep.tile([P, w], U32, name=f"hc{c}_{a}_{m0}", align_bytes=64)
            scale = keep.tile([P, w], U8, name=f"hq{c}_{a}_{m0}", align_bytes=64)
            nc.vector.quantize_mx(codes[:].bitcast(FP8X4), scale[:], h_rounded[c, a][:, PACK * m0 : PACK * (m0 + w)])
            h_mx[c, a] = (codes, scale, m0)

        def second_product(c, m0, w, pool, tag):
            for g in range(N // P):
                y = pool.tile([P, BANK], F32, name=tag)
                for s0 in range(0, w, P):
                    for a in range(PASSES):
                        codes, scale, base = h_mx[c, a]
                        cols = slice(m0 + s0 - base, m0 + s0 - base + P)
                        nc.tensor.matmul_mx(
                            y[:, s0 : s0 + P],
                            lhsT=al_t[:, a, 2 * P * g : 2 * P * (g + 1)].bitcast(FP4X4),
                            lhsT_scale=al_scale[:, a, P * g : P * (g + 1)],
                            rhs=codes[:, cols].bitcast(FP8X4),
                            rhs_scale=scale[:, cols],
                            start=(a == 0),
                            stop=(a == PASSES - 1),
                        )
                y_sums[c, m0, g] = y

        def store(c, m0, w, shared):
            result = keep.tile([P, N // P, w], F32, name=f"res{c}_{m0}")
            first = CHUNKS[c][0] + m0
            for g in range(N // P):
                y = y_sums[c, m0, g]
                if shared and g == 1:
                    nc.vector.tensor_scalar(result[:, g, :], y[:, 0:w], b_t[:, g : g + 1], None, ALU.add)
                else:
                    nc.scalar.activation(result[:, g, :], y[:, 0:w], ACT.Identity, bias=b_t[:, g : g + 1])
            nc.sync.dma_start(out.rearrange("(g p) m -> p g m", p=P)[:, :, first : first + w], result[:])

        x_rounded[1] = keep.tile([P, QUARTER, PACK], BF16, name="xg1", tag="rounded_second_last", align_bytes=64)
        nc.scalar.copy(
            x_rounded[1][:, 0:P, :].rearrange("p (c i) t -> p c t i", i=RUN),
            raw[1][:, :, 0:P].rearrange("p t (c i) -> p c t i", i=RUN),
        )
        nc.gpsimd.tensor_scalar(x_rounded[1][:, P:, :], raw[1][:, :, P:].rearrange("p t m -> p m t"), 1.0, 0.0, ALU.mult, ALU.add)
        first_product(0, 0)
        first_product(0, 1)
        round_x(2, nc.vector.tensor_copy, on_table, offset=rounded_third_at)
        quantize_x(1, 1, on_table, offset=wide_scale_at)
        quantize_x(2, 1)
        round_x(3, nc.vector.tensor_copy, keep, tag="rounded_second_last")
        apply_sign(0, 0)
        first_product(1, 0)
        quantize_x(3, 2, on_scales, offset=2 * QUARTER * PACK)

        interleave_h(0, 0, 0, QUARTER)
        apply_sign(0, 1)
        quantize_h(0, 0, 0, QUARTER)
        interleave_h(0, 1, 0, GPSIMD_COLUMNS, on_gpsimd=True)
        read_vector_row(*VECTOR_ROWS[0])
        read_vector_row(*VECTOR_ROWS[1])
        interleave_h(0, 1, GPSIMD_COLUMNS, QUARTER - GPSIMD_COLUMNS)
        first_product(1, 1)
        apply_sign(1, 0)
        quantize_h(0, 1, 0, QUARTER)
        second_product(0, 0, QUARTER, psum_y, "y")
        store(0, 0, QUARTER, False)
        interleave_h(1, 0, 0, 2 * QUARTER)
        first_product(2, 0)
        apply_sign(1, 1)
        quantize_h(1, 0, 0, 2 * QUARTER)
        first_product(2, 1)

        interleave_h(1, 1, 0, 3 * P)
        interleave_h(1, 1, 3 * P, P, True)
        apply_sign(2, 0)
        interleave_h(2, 0, 0, P, True)
        quantize_h(1, 1, 0, QUARTER)
        second_product(1, 0, QUARTER, psum_y, "y")
        store(1, 0, QUARTER, False)
        interleave_h(2, 0, P, P)
        apply_sign(2, 1)
        interleave_h(2, 1, 0, P)
        quantize_h(1, 1, QUARTER, QUARTER)
        second_product(1, QUARTER, QUARTER, psum_y, "y")
        store(1, QUARTER, QUARTER, False)

        interleave_h(2, 1, P, P)
        quantize_h(2, 0, 0, QUARTER)
        for m0 in (0, P):
            quantize_h(2, 1, m0, P)
            second_product(2, m0, P, psum_d, "d")
        for m0 in (0, P):
            store(2, m0, P, True)
